import numpy as np
import ml_dtypes


def mxq(x, axis, fmt="e4m3"):
    dtype, down = {"e4m3": (ml_dtypes.float8_e4m3fn, 7), "e5m2": (ml_dtypes.float8_e5m2, 14)}[fmt]
    v = np.moveaxis(np.asarray(x, np.float32).astype(ml_dtypes.bfloat16).astype(np.float64), axis, -1)
    blocks = v.reshape(v.shape[:-1] + (-1, 32))
    amax = np.abs(blocks).max(-1, keepdims=True)
    byte = np.maximum(np.where(amax > 0, np.frexp(amax)[1] - 1 + 127, 0) - down, 1)
    scale = np.exp2(byte - 127.0)
    codes = (blocks / scale).astype(np.float32).astype(dtype).astype(np.float64)
    return np.moveaxis((codes * scale).reshape(v.shape), -1, axis)


WIDE = False


def mx_kscale(k):
    if not WIDE:
        return np.ones(k)
    levels = np.array([10, -10, 5, -5, 0])
    if k % 512:
        return np.exp2(np.random.permutation(np.resize(levels, k // 32))).repeat(32)
    a = np.empty((k // 512, 16))
    for p in range(k // 512):
        a[p, :8] = np.random.permutation(np.resize(levels, 8))
        for g in range(8):
            far = levels[np.abs(levels - a[p, g]) >= 10]
            a[p, g + 8] = far[np.random.randint(len(far))]
    return np.exp2(a.ravel()).repeat(32)


BF16 = ml_dtypes.bfloat16


def bf(x):
    return np.asarray(x, np.float32).astype(BF16)


def f64(x):
    return np.asarray(x).astype(np.float64)


E2M1 = np.array([0.0, 0.5, 1.0, 1.5, 2.0, 3.0, 4.0, 6.0, -0.0, -0.5, -1.0, -1.5, -2.0, -3.0, -4.0, -6.0])


def pack_weight(w, fmt):
    k, n = w.shape
    w = f64(bf(w)).reshape(k // 32, 32, n)
    amax = np.abs(w).max(1)
    if fmt == "e4m3":
        byte = np.frexp(amax)[1] - 1 + 127 - 7
    else:
        mant, ex = np.frexp(amax / 6.0)
        byte = np.where(mant > 0.5, ex, ex - 1) + 127
    byte = np.clip(np.where(amax > 0, byte, 1), 1, 254)
    scaled = (w * np.exp2(127.0 - byte)[:, None, :]).reshape(k, n).astype(np.float32)
    by_word = np.ascontiguousarray(scaled.reshape(k // 512, 128, 4, n).transpose(0, 1, 3, 2))
    if fmt == "e4m3":
        words = by_word.astype(ml_dtypes.float8_e4m3fn).view(np.uint8)
    else:
        c = by_word.astype(ml_dtypes.float4_e2m1fn).view(np.uint8) & 0xF
        words = c[..., 0::2] | (c[..., 1::2] << 4)
    return np.ascontiguousarray(words), np.ascontiguousarray(byte.astype(np.uint8).reshape(k // 512, 16, n))


def unpack_weight(words, scales, fmt):
    g, p, n, _ = words.shape
    if fmt == "e4m3":
        vals = np.ascontiguousarray(words).view(ml_dtypes.float8_e4m3fn).astype(np.float64)
    else:
        nib = np.empty((g, p, n, 4), np.uint8)
        nib[..., 0::2] = words & 0xF
        nib[..., 1::2] = words >> 4
        vals = E2M1[nib]
    vals = vals * np.repeat(np.exp2(scales.astype(np.float64) - 127.0), 8, axis=1)[..., None]
    return vals.transpose(0, 1, 3, 2).reshape(g * 512, n)
def pack4(w):
    words, scales = pack_weight(w, "e2m1")
    return words.reshape(words.shape[0], 128, -1), scales


def unpack4(words, scales):
    return unpack_weight(words.reshape(words.shape[0], 128, -1, 2), scales, "e2m1")


S, T, F, C = 512, 4, 1024, 512

BLEED = 0.35


def setup_inputs():
    s = mx_kscale(S)
    t = mx_kscale(F)
    a = BLEED * np.random.standard_normal((S, S)) / np.sqrt(S) / s[:, None]
    l = BLEED * np.random.standard_normal((F, F)) / np.sqrt(F) / t[:, None] * t
    m = np.random.standard_normal((S, C)) / np.sqrt(S) / s[:, None]
    a_words, a_scales = pack4(a)
    l_words, l_scales = pack4(l)
    m_words, m_scales = pack4(m)
    return {"x": bf(np.random.standard_normal((S, T, F)) * s[:, None, None] * t),
            "a_words": a_words, "a_scales": a_scales,
            "l_words": l_words, "l_scales": l_scales,
            "m_words": m_words, "m_scales": m_scales,
            "damp": bf((1 + 0.1 * np.random.standard_normal(S)) * s),
            "resp": bf((1 + 0.1 * np.random.standard_normal(F)) / t),
            "rec": bf(0.5 * np.random.standard_normal((C, T, F)))}


def reference(x, a_words, a_scales, l_words, l_scales, m_words, m_scales, damp, resp, rec):
    A = unpack4(a_words, a_scales)
    L = unpack4(l_words, l_scales)
    M = unpack4(m_words, m_scales)
    x0 = f64(x).reshape(S, T * F)
    b = A.T @ mxq(x0, 0, "e4m3")
    y = (x0 + f64(damp)[:, None] * b).reshape(S * T, F)
    z = y + (mxq(y, 1, "e4m3") @ L)
    v = (M.T @ mxq(z.reshape(S, T * F), 0, "e4m3")).reshape(C, T, F)
    return v * f64(resp) + f64(rec)

@@ -1,0 +1,392 @@
+from contextlib import ExitStack
+
+import concourse.mybir as mybir
+from concourse.masks import make_identity
+
+F32 = mybir.dt.float32
+BF16 = mybir.dt.bfloat16
+U32 = mybir.dt.uint32
+I32 = mybir.dt.int32
+U8 = mybir.dt.uint8
+E4M3 = mybir.dt.float8_e4m3fn_x4
+E2M1 = mybir.dt.float4_e2m1fn_x4
+ADD = mybir.AluOpType.add
+MULT = mybir.AluOpType.mult
+COPY = mybir.ActivationFunctionType.Copy
+
+S, T, F, C = 512, 4, 1024, 512
+P = 128
+W = 512
+HALF_FRAMES = 2 * T
+FLOPS = 2 * (2 * S * S * T * F + S * T * F * F)
+
+VECTOR_BANKS = 5
+SCALAR_BANKS = 3
+RESULTS = 8
+
+ROUND = (
+    ("interleave", (0,), 1),
+    ("add_record", (2, 3), 11),
+    ("add_record_gpsimd", (1,), 11),
+    ("respond", (0, 1), 9),
+    ("quantise_z", (0,), 8),
+    ("interleave", (1,), 0),
+    ("leak", (0, 1), 7),
+    ("copy_out", (1,), 10),
+    ("turn_y", (0,), 4),
+    ("bleed_matmul", (2, 3), 3),
+    ("round_y", (0,), 3),
+    ("add_record", (0, 1), 10),
+    ("mix_matmul", (2, 3), 9),
+    ("quantise_x", (0,), 1),
+    ("gather_y", (0,), 4),
+    ("respond", (2, 3), 9),
+    ("leak_matmul", (2, 3), 7),
+    ("bleed", (2, 3), 3),
+    ("turn_y", (2,), 4),
+    ("turn_back", (2, 3), 10),
+    ("gather_y", (2,), 4),
+    ("quantise_y", (0,), 5),
+    ("leak", (2, 3), 7),
+    ("round_y", (2,), 3),
+    ("bleed_matmul", (0, 1), 2),
+    ("mix_matmul", (0, 1), 8),
+    ("copy_out", (3,), 10),
+    ("bleed", (0, 1), 2),
+    ("leak_matmul", (0, 1), 6),
+    ("turn_back", (0, 1), 9),
+    ("add_record_gpsimd", (3,), 12),
+)
+
+
+def tile_orchestra_bleed_mix_t2_kernel(
+    tc, x, a_words, a_scales, l_words, l_scales, m_words, m_scales, damp, resp, rec, out
+):
+    nc = tc.nc
+    with ExitStack() as ctx:
+        keep = ctx.enter_context(tc.tile_pool(name="keep", bufs=1))
+        work = ctx.enter_context(tc.tile_pool(name="work", bufs=2))
+        psum = ctx.enter_context(tc.psum_pool(name="psum", bufs=1))
+        ctx.enter_context(tc.manual_schedule())
+
+        a_arrived = keep.tile([P, 2 * S], U8, align_bytes=64)
+        a_scales_arrived = keep.tile([P, S], U8, align_bytes=64)
+        a_codes = keep.tile([P, 2 * S], U8, align_bytes=64)
+        a_plane = keep.tile([P, S], U8, align_bytes=64)
+        l_codes = keep.tile([P, 2, 2 * F], U8, align_bytes=64)
+        l_plane = keep.tile([P, 2, F], U8, align_bytes=64)
+        m_codes = keep.tile([P, 2 * C], U8, align_bytes=64)
+        m_plane = keep.tile([P, C], U8, align_bytes=64)
+        damp_col = keep.tile([P, 4], BF16)
+        resp_rows = keep.tile([P, P], BF16, align_bytes=64)
+        resp_col = keep.tile([P, F // P], F32)
+        ident = keep.tile([P, P], F32, align_bytes=64)
+        ident_bf16 = keep.tile([P, P], BF16, align_bytes=64)
+        raw = []
+        for r in range(T):
+            raw_r = keep.tile([P, 4, F], BF16, align_bytes=64, name="raw%d" % r)
+            raw.append(raw_r)
+
+        def as_int32(ap):
+            return ap.bitcast(I32)
+
+        def on_gpsimd(u, m):
+            return u < 5 and m % 2 == 1
+
+        nc.vector.memset(as_int32(a_scales_arrived[:]), 0)
+        make_identity(nc, ident[:])
+        nc.gpsimd.memset(resp_rows[:], 0.0)
+        make_identity(nc, ident_bf16[:])
+        nc.gpsimd.memset(as_int32(l_plane[:]), 0)
+        nc.gpsimd.memset(as_int32(m_plane[:]), 0)
+
+        def load_x(r, f0, f1, queue=nc.sync):
+            queue.dma_start(out=raw[r][:, :, f0:f1], in_=x.rearrange("(p t) r f -> p t r f", t=4)[:, :, r, f0:f1])
+
+        recs = {}
+
+        def load_rec(r):
+            recs[r] = work.tile([P, C // P, F], BF16, align_bytes=64, name="rec", bufs=3)
+            nc.sync.dma_start(out=recs[r][:], in_=rec.rearrange("(m c) r f -> c m r f", c=P)[:, :, r, :])
+
+        load_x(0, 0, W, nc.scalar)
+        nc.sync.dma_start(out=as_int32(a_arrived[:]), in_=as_int32(a_words[0]))
+        for q in range(4):
+            nc.sync.dma_start(
+                out=as_int32(a_scales_arrived[32 * q : 32 * q + 4, :]),
+                in_=as_int32(a_scales[0, 4 * q : 4 * q + 4, :]),
+            )
+        load_x(0, W, F)
+        nc.sync.dma_start(out=damp_col[:], in_=damp.rearrange("(p t) -> p t", t=4))
+        load_x(1, 0, F)
+        nc.sync.dma_start(out=as_int32(l_codes[:]), in_=as_int32(l_words.rearrange("g p n -> p g n")))
+        for q in range(4):
+            nc.sync.dma_start(
+                out=as_int32(l_plane[32 * q : 32 * q + 4, :, :]),
+                in_=as_int32(l_scales[:, 4 * q : 4 * q + 4, :].rearrange("g q n -> q g n")),
+            )
+        load_x(2, 0, F)
+        nc.sync.dma_start(out=resp_rows[0 : F // P, :], in_=resp.rearrange("(b q) -> b q", q=P))
+        nc.sync.dma_start(out=as_int32(m_codes[:]), in_=as_int32(m_words[0]))
+        for q in range(4):
+            nc.sync.dma_start(
+                out=as_int32(m_plane[32 * q : 32 * q + 4, :]), in_=as_int32(m_scales[0, 4 * q : 4 * q + 4, :])
+            )
+        load_x(3, 0, F)
+        for r in range(3):
+            load_rec(r)
+
+        def reorder_a(half):
+            ts = slice(2 * half, 2 * half + 2)
+            nc.vector.tensor_copy(
+                out=a_codes[:].rearrange("p (t m b) -> p t m b", t=4, b=2)[:, ts],
+                in_=a_arrived[:].rearrange("p (m t b) -> p t m b", t=4, b=2)[:, ts],
+            )
+            nc.vector.tensor_copy(
+                out=a_plane[:].rearrange("p (t m) -> p t m", t=4)[:, ts],
+                in_=a_scales_arrived[:].rearrange("p (m t) -> p t m", t=4)[:, ts],
+            )
+
+        reorder_a(0)
+
+        grouped, x_codes, x_plane = {}, {}, {}
+        y, y_bf16, y_turned, y_codes, y_plane = {}, {}, {}, {}, {}
+        z, z_codes, z_plane, scaled, copied, bank_of = {}, {}, {}, {}, {}, {}
+
+        def interleave(u, half):
+            r, g = divmod(u, 2)
+            if r not in grouped:
+                grouped[r] = work.tile([P, 2, W, 4], BF16, align_bytes=64, name="grouped")
+            width = W // 2 if u == 0 else W // 4
+            for f0 in range(half * W // 2, (half + 1) * W // 2, width):
+                out_ap = grouped[r][:, g, f0 : f0 + width, :]
+                in_ap = raw[r][:, :, g * W + f0 : g * W + f0 + width]
+                if half == 0 and u >= 2:
+                    nc.gpsimd.tensor_scalar(
+                        out=out_ap, in0=in_ap.rearrange("p t f -> p f t"), scalar1=1.0, scalar2=0.0, op0=MULT, op1=ADD
+                    )
+                else:
+                    copy = nc.vector.tensor_copy if (u, half) == (0, 0) else nc.scalar.copy
+                    copy(
+                        out=out_ap.rearrange("p (c i) t -> p c t i", i=4),
+                        in_=in_ap.rearrange("p t (c i) -> p c t i", i=4),
+                    )
+            if (u, half) == (0, 0):
+                reorder_a(1)
+
+        def quantise_x(u):
+            r, g = divmod(u, 2)
+            if r not in x_codes:
+                x_codes[r] = work.tile([P, 2, W], U32, align_bytes=64, name="x_codes")
+                x_plane[r] = work.tile([P, 2, W], U8, align_bytes=64, name="x_plane")
+            if r > 0 and g == 0:
+                return
+            gs = slice(0 if r else g, g + 1)
+            nc.vector.quantize_mx(
+                out=x_codes[r][:, gs, :].rearrange("p g f -> p (g f)").bitcast(E4M3),
+                scales=x_plane[r][:, gs, :].rearrange("p g f -> p (g f)"),
+                in_=grouped[r][:, gs].rearrange("p g f t -> p (g f t)"),
+            )
+
+        def bleed_matmul(u, t):
+            r, g = divmod(u, 2)
+            bank = psum.tile([P, W], F32, name="for_vector", bufs=VECTOR_BANKS)
+            bank_of["bleed", u, t] = bank
+            nc.tensor.matmul_mx(
+                out=bank[:],
+                lhsT=a_codes[:, 2 * P * t : 2 * P * (t + 1)].bitcast(E2M1),
+                lhsT_scale=a_plane[:, P * t : P * (t + 1)],
+                rhs=x_codes[r][:, g, :].bitcast(E4M3),
+                rhs_scale=x_plane[r][:, g, :],
+                start=True,
+                stop=True,
+            )
+
+        def bleed(u, t):
+            r, g = divmod(u, 2)
+            fs = slice(g * W, (g + 1) * W)
+            if r not in y:
+                y[r] = work.tile([P, 4, F], F32, align_bytes=64, name="y", bufs=3)
+            nc.vector.scalar_tensor_tensor(
+                out=y[r][:, t, fs],
+                in0=bank_of["bleed", u, t][:],
+                scalar=damp_col[:, t : t + 1],
+                in1=raw[r][:, t, fs],
+                op0=MULT,
+                op1=ADD,
+            )
+
+        def round_y(u, t):
+            r, g = divmod(u, 2)
+            if u not in y_bf16:
+                y_bf16[u] = work.tile([P, 4 * W], BF16, align_bytes=64, name="y_bf16")
+            nc.scalar.copy(
+                out=y_bf16[u][:, W * t : W * (t + 2)].rearrange("p (t h w e) -> p t h w e", t=2, h=2, e=2),
+                in_=y[r][:, t : t + 2, g * W : (g + 1) * W].rearrange("p t (w h e) -> p t h w e", h=2, e=2),
+            )
+
+        def turn_y(u, t):
+            bank = psum.tile([P, 2, 2, P], F32, name="for_scalar", bufs=SCALAR_BANKS)
+            bank_of["turn", u, t] = bank
+            for dt in range(2):
+                for h in range(2):
+                    first = W * (t + dt) + W // 2 * h
+                    pairs = y_bf16[u][:, first : first + W // 2].bitcast(F32)
+                    nc.tensor.transpose(bank[:, dt, h, :], pairs, ident[:])
+
+        def gather_y(u, t):
+            r, g = divmod(u, 2)
+            if r not in y_turned:
+                y_turned[r] = work.tile([P, 2 * 4 * S], BF16, align_bytes=64, name="y_turned")
+            pairs = y_turned[r][:].bitcast(F32).rearrange("p (g t j h) -> p g t j h", g=2, t=4, h=2)
+            nc.scalar.copy(
+                out=pairs[:, g, t : t + 2], in_=bank_of["turn", u, t][:].rearrange("p t h j -> p t j h")
+            )
+
+        def quantise_y(u):
+            r, g = divmod(u, 2)
+            if r not in y_codes:
+                y_codes[r] = work.tile([P, 2, S], U32, align_bytes=64, name="y_codes")
+                y_plane[r] = work.tile([P, 2, S], U8, align_bytes=64, name="y_plane")
+            if r > 0 and g == 0:
+                return
+            gs = slice(0 if r else g, g + 1)
+            nc.vector.quantize_mx(
+                out=y_codes[r][:, gs, :].rearrange("p g j -> p (g j)").bitcast(E4M3),
+                scales=y_plane[r][:, gs, :].rearrange("p g j -> p (g j)"),
+                in_=y_turned[r][:, 4 * S * gs.start : 4 * S * gs.stop],
+            )
+
+        def leak_matmul(u, k):
+            r, b = u // 2, 4 * (u % 2) + k
+            bank = psum.tile([P, 4, P], F32, name="for_vector", bufs=VECTOR_BANKS)
+            bank_of["leak", u, k] = bank
+            for t in range(4):
+                for g in range(2):
+                    nc.tensor.matmul_mx(
+                        out=bank[:, t, :],
+                        lhsT=y_codes[r][:, g, P * t : P * (t + 1)].bitcast(E4M3),
+                        lhsT_scale=y_plane[r][:, g, P * t : P * (t + 1)],
+                        rhs=l_codes[:, g, 2 * P * b : 2 * P * (b + 1)].bitcast(E2M1),
+                        rhs_scale=l_plane[:, g, P * b : P * (b + 1)],
+                        start=(g == 0),
+                        stop=(g == 1),
+                    )
+
+        def leak(u, k):
+            r, b = u // 2, 4 * (u % 2) + k
+            if u not in z:
+                z[u] = work.tile([P, W, 4], BF16, align_bytes=64, name="z", bufs=3)
+            nc.vector.tensor_tensor(
+                out=z[u][:, P * k : P * (k + 1), :].rearrange("p (c i) t -> p c t i", i=2),
+                in0=bank_of["leak", u, k][:].rearrange("p t (c i) -> p c t i", i=2),
+                in1=y[r][:, :, P * b : P * (b + 1)].rearrange("p t (c i) -> p c t i", i=2),
+                op=ADD,
+            )
+
+        def quantise_z(u):
+            z_codes[u] = work.tile([P, W], U32, align_bytes=64, name="z_codes", bufs=3)
+            z_plane[u] = work.tile([P, W], U8, align_bytes=64, name="z_plane", bufs=3)
+            nc.vector.quantize_mx(
+                out=z_codes[u][:].bitcast(E4M3), scales=z_plane[u][:], in_=z[u][:].rearrange("p f t -> p (f t)")
+            )
+
+        def turn_resp():
+            bank = psum.tile([P, P], BF16, name="for_scalar", bufs=SCALAR_BANKS)
+            nc.tensor.transpose(bank[:], resp_rows[:], ident_bf16[:])
+            nc.scalar.copy(out=resp_col[:], in_=bank[:, 0 : F // P])
+
+        def mix_matmul(u, k):
+            if (u, k) == (0, 0):
+                turn_resp()
+            bank = psum.tile([P, C], F32, name="for_scalar", bufs=SCALAR_BANKS)
+            bank_of["mix", u, k] = bank
+            nc.tensor.matmul_mx(
+                out=bank[:],
+                lhsT=z_codes[u][:, P * k : P * (k + 1)].bitcast(E4M3),
+                lhsT_scale=z_plane[u][:, P * k : P * (k + 1)],
+                rhs=m_codes[:].bitcast(E2M1),
+                rhs_scale=m_plane[:],
+                start=True,
+                stop=True,
+            )
+
+        def respond(u, k):
+            if u not in scaled:
+                scaled[u] = work.tile([P, 4, C], F32, align_bytes=64, name="scaled")
+            b = 4 * (u % 2) + k
+            nc.scalar.activation(
+                out=scaled[u][:, k, :], in_=bank_of["mix", u, k][:], func=COPY, scale=resp_col[:, b : b + 1]
+            )
+
+        def turn_back(u, m):
+            if on_gpsimd(u, m):
+                bank = psum.tile([P, 4, P], F32, name="for_scalar", bufs=SCALAR_BANKS)
+            else:
+                bank = psum.tile([P, 4, P], F32, name="for_vector", bufs=VECTOR_BANKS)
+            bank_of["back", u, m] = bank
+            for k in range(4):
+                nc.tensor.transpose(bank[:, k, :], scaled[u][:, k, P * m : P * (m + 1)], ident[:])
+
+        def store(u, m, result):
+            r, g = divmod(u, 2)
+            nc.sync.dma_start(out=out[P * m : P * (m + 1), r, g * W : (g + 1) * W], in_=result[:])
+            if u == 3 and 3 not in recs:
+                load_rec(3)
+
+        def copy_out(u, m):
+            if on_gpsimd(u, m):
+                copied[u, m] = work.tile([P, W], F32, name="copied", bufs=3)
+                nc.scalar.copy(out=copied[u, m][:], in_=bank_of["back", u, m][:].rearrange("p k f -> p (k f)"))
+
+        def add_record_gpsimd(u, m):
+            if on_gpsimd(u, m):
+                r, g = divmod(u, 2)
+                result = work.tile([P, W], F32, name="result", bufs=RESULTS)
+                for f0 in range(0, W, W // 2):
+                    nc.gpsimd.tensor_tensor(
+                        out=result[:, f0 : f0 + W // 2],
+                        in0=copied[u, m][:, f0 : f0 + W // 2],
+                        in1=recs[r][:, m, g * W + f0 : g * W + f0 + W // 2],
+                        op=ADD,
+                    )
+                store(u, m, result)
+
+        def add_record(u, m):
+            if on_gpsimd(u, m):
+                return
+            r, g = divmod(u, 2)
+            result = work.tile([P, W], F32, name="result", bufs=RESULTS)
+            nc.vector.tensor_tensor(
+                out=result[:],
+                in0=bank_of["back", u, m][:].rearrange("p k f -> p (k f)"),
+                in1=recs[r][:, m, g * W : (g + 1) * W],
+                op=ADD,
+            )
+            store(u, m, result)
+
+        stages = {
+            "interleave": interleave,
+            "quantise_x": lambda u, i: quantise_x(u),
+            "bleed_matmul": bleed_matmul,
+            "bleed": bleed,
+            "round_y": round_y,
+            "turn_y": turn_y,
+            "gather_y": gather_y,
+            "quantise_y": lambda u, i: quantise_y(u),
+            "leak_matmul": leak_matmul,
+            "leak": leak,
+            "quantise_z": lambda u, i: quantise_z(u),
+            "mix_matmul": mix_matmul,
+            "respond": respond,
+            "turn_back": turn_back,
+            "add_record": add_record,
+            "copy_out": copy_out,
+            "add_record_gpsimd": add_record_gpsimd,
+        }
+        last_lag = max(lag for stage, steps, lag in ROUND)
+        for h in range(HALF_FRAMES + last_lag):
+            for stage, steps, lag in ROUND:
+                if 0 <= h - lag < HALF_FRAMES:
+                    for i in steps:
+                        stages[stage](h - lag, i)

@@ -7,6 +7,7 @@ F32 = mybir.dt.float32
 BF16 = mybir.dt.bfloat16
 U32 = mybir.dt.uint32
 I32 = mybir.dt.int32
+U16 = mybir.dt.uint16
 U8 = mybir.dt.uint8
 E4M3 = mybir.dt.float8_e4m3fn_x4
 E2M1 = mybir.dt.float4_e2m1fn_x4
@@ -20,43 +21,13 @@ W = 512
 HALF_FRAMES = 2 * T
 FLOPS = 2 * (2 * S * S * T * F + S * T * F * F)
 
-VECTOR_BANKS = 5
-SCALAR_BANKS = 3
+Q = 256
+QUARTERS = 4 * T
+BANKS = 8
 RESULTS = 8
-
-ROUND = (
-    ("interleave", (0,), 1),
-    ("add_record", (2, 3), 11),
-    ("add_record_gpsimd", (1,), 11),
-    ("respond", (0, 1), 9),
-    ("quantise_z", (0,), 8),
-    ("interleave", (1,), 0),
-    ("leak", (0, 1), 7),
-    ("copy_out", (1,), 10),
-    ("turn_y", (0,), 4),
-    ("bleed_matmul", (2, 3), 3),
-    ("round_y", (0,), 3),
-    ("add_record", (0, 1), 10),
-    ("mix_matmul", (2, 3), 9),
-    ("quantise_x", (0,), 1),
-    ("gather_y", (0,), 4),
-    ("respond", (2, 3), 9),
-    ("leak_matmul", (2, 3), 7),
-    ("bleed", (2, 3), 3),
-    ("turn_y", (2,), 4),
-    ("turn_back", (2, 3), 10),
-    ("gather_y", (2,), 4),
-    ("quantise_y", (0,), 5),
-    ("leak", (2, 3), 7),
-    ("round_y", (2,), 3),
-    ("bleed_matmul", (0, 1), 2),
-    ("mix_matmul", (0, 1), 8),
-    ("copy_out", (3,), 10),
-    ("bleed", (0, 1), 2),
-    ("leak_matmul", (0, 1), 6),
-    ("turn_back", (0, 1), 9),
-    ("add_record_gpsimd", (3,), 12),
-)
+SHARED = 6
+GPSIMD_QUARTERS = 8
+GPSIMD_BINS = 192
 
 
 def tile_orchestra_bleed_mix_t2_kernel(
@@ -69,36 +40,41 @@ def tile_orchestra_bleed_mix_t2_kernel(
         psum = ctx.enter_context(tc.psum_pool(name="psum", bufs=1))
         ctx.enter_context(tc.manual_schedule())
 
-        a_arrived = keep.tile([P, 2 * S], U8, align_bytes=64)
-        a_scales_arrived = keep.tile([P, S], U8, align_bytes=64)
-        a_codes = keep.tile([P, 2 * S], U8, align_bytes=64)
-        a_plane = keep.tile([P, S], U8, align_bytes=64)
-        l_codes = keep.tile([P, 2, 2 * F], U8, align_bytes=64)
-        l_plane = keep.tile([P, 2, F], U8, align_bytes=64)
-        m_codes = keep.tile([P, 2 * C], U8, align_bytes=64)
-        m_plane = keep.tile([P, C], U8, align_bytes=64)
-        damp_col = keep.tile([P, 4], BF16)
-        resp_rows = keep.tile([P, P], BF16, align_bytes=64)
-        resp_col = keep.tile([P, F // P], F32)
-        ident = keep.tile([P, P], F32, align_bytes=64)
-        ident_bf16 = keep.tile([P, P], BF16, align_bytes=64)
+        a_arrived = keep.tile([P, 2 * S], U8, align_bytes=64, name="a_arrived")
+        a_scales_arrived = keep.tile([P, S], U8, align_bytes=64, name="a_scales_arrived")
+        a_codes = keep.tile([P, 2 * S], U8, align_bytes=64, name="a_codes")
+        a_plane = keep.tile([P, S], U8, align_bytes=64, name="a_plane")
+        l_codes = keep.tile([P, 2, 2 * F], U8, align_bytes=64, name="l_codes")
+        l_plane = keep.tile([P, 2, F], U8, align_bytes=64, name="l_plane")
+        m_codes = keep.tile([P, 2 * C], U8, align_bytes=64, name="m_codes")
+        m_plane = keep.tile([P, C], U8, align_bytes=64, name="m_plane")
+        damp_col = keep.tile([P, 4], BF16, name="damp_col")
+        resp_rows = keep.tile([P, P], BF16, align_bytes=64, name="resp_rows")
+        resp_wide = keep.tile([P, P], F32, align_bytes=64, name="resp_wide")
+        resp_col = keep.tile([P, F // P], F32, name="resp_col")
+        ident = keep.tile([P, P], F32, align_bytes=64, name="ident")
         raw = []
         for r in range(T):
             raw_r = keep.tile([P, 4, F], BF16, align_bytes=64, name="raw%d" % r)
             raw.append(raw_r)
 
+        shared = []
+        for i in range(SHARED):
+            shared_i = keep.tile([P, W], F32, align_bytes=64, name="shared%d" % i)
+            shared.append(shared_i)
+
         def as_int32(ap):
             return ap.bitcast(I32)
 
-        def on_gpsimd(u, m):
-            return u < 5 and m % 2 == 1
+        def on_gpsimd(n, m):
+            return n < GPSIMD_QUARTERS and m == 2
 
         nc.vector.memset(as_int32(a_scales_arrived[:]), 0)
-        make_identity(nc, ident[:])
-        nc.gpsimd.memset(resp_rows[:], 0.0)
-        make_identity(nc, ident_bf16[:])
-        nc.gpsimd.memset(as_int32(l_plane[:]), 0)
-        nc.gpsimd.memset(as_int32(m_plane[:]), 0)
+        nc.vector.memset(ident[:], 0.0)
+        nc.vector.memset(as_int32(l_plane[:]), 0)
+        nc.vector.memset(as_int32(m_plane[:]), 0)
+        nc.vector.memset(resp_rows[:], 0.0)
+        make_identity(nc, ident[:], nomemset=True)
 
         def load_x(r, f0, f1, queue=nc.sync):
             queue.dma_start(out=raw[r][:, :, f0:f1], in_=x.rearrange("(p t) r f -> p t r f", t=4)[:, :, r, f0:f1])
@@ -136,137 +112,118 @@ def tile_orchestra_bleed_mix_t2_kernel(
         for r in range(3):
             load_rec(r)
 
-        def reorder_a(half):
-            ts = slice(2 * half, 2 * half + 2)
+        def reorder_a():
             nc.vector.tensor_copy(
-                out=a_codes[:].rearrange("p (t m b) -> p t m b", t=4, b=2)[:, ts],
-                in_=a_arrived[:].rearrange("p (m t b) -> p t m b", t=4, b=2)[:, ts],
+                out=a_codes[:].bitcast(U16).rearrange("p (t m) -> p t m", t=4),
+                in_=a_arrived[:].bitcast(U16).rearrange("p (m t) -> p t m", t=4),
             )
             nc.vector.tensor_copy(
-                out=a_plane[:].rearrange("p (t m) -> p t m", t=4)[:, ts],
-                in_=a_scales_arrived[:].rearrange("p (m t) -> p t m", t=4)[:, ts],
+                out=a_plane[:].rearrange("p (t m) -> p t m", t=4),
+                in_=a_scales_arrived[:].rearrange("p (m t) -> p t m", t=4),
             )
-
-        reorder_a(0)
 
         grouped, x_codes, x_plane = {}, {}, {}
         y, y_bf16, y_turned, y_codes, y_plane = {}, {}, {}, {}, {}
-        z, z_codes, z_plane, scaled, copied, bank_of = {}, {}, {}, {}, {}, {}
+        z_codes, z_plane, scaled, copied, bank_of = {}, {}, {}, {}, {}
 
-        def interleave(u, half):
-            r, g = divmod(u, 2)
-            if r not in grouped:
-                grouped[r] = work.tile([P, 2, W, 4], BF16, align_bytes=64, name="grouped")
-            width = W // 2 if u == 0 else W // 4
-            for f0 in range(half * W // 2, (half + 1) * W // 2, width):
-                out_ap = grouped[r][:, g, f0 : f0 + width, :]
-                in_ap = raw[r][:, :, g * W + f0 : g * W + f0 + width]
-                if half == 0 and u >= 2:
-                    nc.gpsimd.tensor_scalar(
-                        out=out_ap, in0=in_ap.rearrange("p t f -> p f t"), scalar1=1.0, scalar2=0.0, op0=MULT, op1=ADD
-                    )
-                else:
-                    copy = nc.vector.tensor_copy if (u, half) == (0, 0) else nc.scalar.copy
-                    copy(
-                        out=out_ap.rearrange("p (c i) t -> p c t i", i=4),
-                        in_=in_ap.rearrange("p t (c i) -> p c t i", i=4),
-                    )
-            if (u, half) == (0, 0):
-                reorder_a(1)
+        def interleave(n, f0, f1, engine):
+            if n not in grouped:
+                name, bufs = ("grouped_early", 4) if n < 6 else ("grouped", 1)
+                grouped[n] = work.tile([P, Q, 4], BF16, align_bytes=64, name=name, bufs=bufs)
+            out_ap = grouped[n][:, f0:f1, :]
+            in_ap = raw[n // 4][:, :, Q * (n % 4) + f0 : Q * (n % 4) + f1]
+            if engine == "gpsimd":
+                nc.gpsimd.tensor_scalar(
+                    out=out_ap, in0=in_ap.rearrange("p t f -> p f t"), scalar1=1.0, scalar2=0.0, op0=MULT, op1=ADD
+                )
+            else:
+                copy = nc.vector.tensor_copy if engine == "vector" else nc.scalar.copy
+                copy(
+                    out=out_ap.rearrange("p (c i) t -> p c t i", i=4),
+                    in_=in_ap.rearrange("p t (c i) -> p c t i", i=4),
+                )
 
-        def quantise_x(u):
-            r, g = divmod(u, 2)
-            if r not in x_codes:
-                x_codes[r] = work.tile([P, 2, W], U32, align_bytes=64, name="x_codes")
-                x_plane[r] = work.tile([P, 2, W], U8, align_bytes=64, name="x_plane")
-            if r > 0 and g == 0:
-                return
-            gs = slice(0 if r else g, g + 1)
+        def quantise_x(n):
+            u, j = divmod(n, 2)
+            if u not in x_codes:
+                x_codes[u] = work.tile([P, W], U32, align_bytes=64, name="x_codes", bufs=3)
+                x_plane[u] = work.tile([P, W], U8, align_bytes=64, name="x_plane", bufs=3)
             nc.vector.quantize_mx(
-                out=x_codes[r][:, gs, :].rearrange("p g f -> p (g f)").bitcast(E4M3),
-                scales=x_plane[r][:, gs, :].rearrange("p g f -> p (g f)"),
-                in_=grouped[r][:, gs].rearrange("p g f t -> p (g f t)"),
+                out=x_codes[u][:, Q * j : Q * (j + 1)].bitcast(E4M3),
+                scales=x_plane[u][:, Q * j : Q * (j + 1)],
+                in_=grouped[n][:].rearrange("p f t -> p (f t)"),
             )
 
+        def next_bank():
+            return psum.tile([P, W], F32, name="bank", bufs=BANKS)
+
         def bleed_matmul(u, t):
-            r, g = divmod(u, 2)
-            bank = psum.tile([P, W], F32, name="for_vector", bufs=VECTOR_BANKS)
+            bank = next_bank()
             bank_of["bleed", u, t] = bank
             nc.tensor.matmul_mx(
                 out=bank[:],
                 lhsT=a_codes[:, 2 * P * t : 2 * P * (t + 1)].bitcast(E2M1),
                 lhsT_scale=a_plane[:, P * t : P * (t + 1)],
-                rhs=x_codes[r][:, g, :].bitcast(E4M3),
-                rhs_scale=x_plane[r][:, g, :],
+                rhs=x_codes[u][:].bitcast(E4M3),
+                rhs_scale=x_plane[u][:],
                 start=True,
                 stop=True,
             )
 
         def bleed(u, t):
             r, g = divmod(u, 2)
-            fs = slice(g * W, (g + 1) * W)
-            if r not in y:
-                y[r] = work.tile([P, 4, F], F32, align_bytes=64, name="y", bufs=3)
+            if u not in y:
+                y[u] = work.tile([P, 4, W], F32, align_bytes=64, name="y", bufs=5)
             nc.vector.scalar_tensor_tensor(
-                out=y[r][:, t, fs],
+                out=y[u][:, t, :],
                 in0=bank_of["bleed", u, t][:],
                 scalar=damp_col[:, t : t + 1],
-                in1=raw[r][:, t, fs],
+                in1=raw[r][:, t, g * W : (g + 1) * W],
                 op0=MULT,
                 op1=ADD,
             )
 
         def round_y(u, t):
-            r, g = divmod(u, 2)
-            if u not in y_bf16:
-                y_bf16[u] = work.tile([P, 4 * W], BF16, align_bytes=64, name="y_bf16")
+            y_bf16[u, t] = work.tile([P, 2 * W], BF16, align_bytes=64, name="y_bf16", bufs=3)
             nc.scalar.copy(
-                out=y_bf16[u][:, W * t : W * (t + 2)].rearrange("p (t h w e) -> p t h w e", t=2, h=2, e=2),
-                in_=y[r][:, t : t + 2, g * W : (g + 1) * W].rearrange("p t (w h e) -> p t h w e", h=2, e=2),
+                out=y_bf16[u, t][:].rearrange("p (t h w e) -> p t h w e", t=2, h=2, e=2),
+                in_=y[u][:, t : t + 2, :].rearrange("p t (w h e) -> p t h w e", h=2, e=2),
             )
 
         def turn_y(u, t):
-            bank = psum.tile([P, 2, 2, P], F32, name="for_scalar", bufs=SCALAR_BANKS)
+            bank = next_bank()
             bank_of["turn", u, t] = bank
-            for dt in range(2):
-                for h in range(2):
-                    first = W * (t + dt) + W // 2 * h
-                    pairs = y_bf16[u][:, first : first + W // 2].bitcast(F32)
-                    nc.tensor.transpose(bank[:, dt, h, :], pairs, ident[:])
+            for j in range(4):
+                pairs = y_bf16[u, t][:, 2 * P * j : 2 * P * (j + 1)].bitcast(F32)
+                nc.tensor.transpose(bank[:, P * j : P * (j + 1)], pairs, ident[:])
 
         def gather_y(u, t):
-            r, g = divmod(u, 2)
-            if r not in y_turned:
-                y_turned[r] = work.tile([P, 2 * 4 * S], BF16, align_bytes=64, name="y_turned")
-            pairs = y_turned[r][:].bitcast(F32).rearrange("p (g t j h) -> p g t j h", g=2, t=4, h=2)
+            y_turned[u, t] = work.tile([P, 2 * S], BF16, align_bytes=64, name="y_turned", bufs=3)
             nc.scalar.copy(
-                out=pairs[:, g, t : t + 2], in_=bank_of["turn", u, t][:].rearrange("p t h j -> p t j h")
+                out=y_turned[u, t][:].bitcast(F32).rearrange("p (t j h) -> p t j h", t=2, h=2),
+                in_=bank_of["turn", u, t][:].rearrange("p (t h j) -> p t j h", t=2, h=2),
             )
 
-        def quantise_y(u):
-            r, g = divmod(u, 2)
-            if r not in y_codes:
-                y_codes[r] = work.tile([P, 2, S], U32, align_bytes=64, name="y_codes")
-                y_plane[r] = work.tile([P, 2, S], U8, align_bytes=64, name="y_plane")
-            if r > 0 and g == 0:
-                return
-            gs = slice(0 if r else g, g + 1)
+        def quantise_y(u, t):
+            if u not in y_codes:
+                y_codes[u] = work.tile([P, S], U32, align_bytes=64, name="y_codes", bufs=4)
+                y_plane[u] = work.tile([P, S], U8, align_bytes=64, name="y_plane", bufs=4)
             nc.vector.quantize_mx(
-                out=y_codes[r][:, gs, :].rearrange("p g j -> p (g j)").bitcast(E4M3),
-                scales=y_plane[r][:, gs, :].rearrange("p g j -> p (g j)"),
-                in_=y_turned[r][:, 4 * S * gs.start : 4 * S * gs.stop],
+                out=y_codes[u][:, P * t : P * (t + 2)].bitcast(E4M3),
+                scales=y_plane[u][:, P * t : P * (t + 2)],
+                in_=y_turned[u, t][:],
             )
 
         def leak_matmul(u, k):
             r, b = u // 2, 4 * (u % 2) + k
-            bank = psum.tile([P, 4, P], F32, name="for_vector", bufs=VECTOR_BANKS)
+            bank = next_bank()
             bank_of["leak", u, k] = bank
             for t in range(4):
                 for g in range(2):
                     nc.tensor.matmul_mx(
-                        out=bank[:, t, :],
-                        lhsT=y_codes[r][:, g, P * t : P * (t + 1)].bitcast(E4M3),
-                        lhsT_scale=y_plane[r][:, g, P * t : P * (t + 1)],
+                        out=bank[:, P * t : P * (t + 1)],
+                        lhsT=y_codes[2 * r + g][:, P * t : P * (t + 1)].bitcast(E4M3),
+                        lhsT_scale=y_plane[2 * r + g][:, P * t : P * (t + 1)],
                         rhs=l_codes[:, g, 2 * P * b : 2 * P * (b + 1)].bitcast(E2M1),
                         rhs_scale=l_plane[:, g, P * b : P * (b + 1)],
                         start=(g == 0),
@@ -274,37 +231,38 @@ def tile_orchestra_bleed_mix_t2_kernel(
                     )
 
         def leak(u, k):
-            r, b = u // 2, 4 * (u % 2) + k
-            if u not in z:
-                z[u] = work.tile([P, W, 4], BF16, align_bytes=64, name="z", bufs=3)
+            half = shared[(2 * u + k // 2) % SHARED][:, Q * (k % 2) : Q * (k % 2 + 1)].bitcast(BF16)
             nc.vector.tensor_tensor(
-                out=z[u][:, P * k : P * (k + 1), :].rearrange("p (c i) t -> p c t i", i=2),
-                in0=bank_of["leak", u, k][:].rearrange("p t (c i) -> p c t i", i=2),
-                in1=y[r][:, :, P * b : P * (b + 1)].rearrange("p t (c i) -> p c t i", i=2),
+                out=half.rearrange("p (c i t) -> p c t i", i=2, t=4),
+                in0=bank_of["leak", u, k][:].rearrange("p (t c i) -> p c t i", t=4, i=2),
+                in1=y[u][:, :, P * k : P * (k + 1)].rearrange("p t (c i) -> p c t i", i=2),
                 op=ADD,
             )
 
-        def quantise_z(u):
-            z_codes[u] = work.tile([P, W], U32, align_bytes=64, name="z_codes", bufs=3)
-            z_plane[u] = work.tile([P, W], U8, align_bytes=64, name="z_plane", bufs=3)
+        def quantise_z(u, k):
+            z_codes[u, k] = work.tile([P, 2 * P], U32, align_bytes=64, name="z_codes", bufs=3)
+            z_plane[u, k] = work.tile([P, 2 * P], U8, align_bytes=64, name="z_plane", bufs=3)
             nc.vector.quantize_mx(
-                out=z_codes[u][:].bitcast(E4M3), scales=z_plane[u][:], in_=z[u][:].rearrange("p f t -> p (f t)")
+                out=z_codes[u, k][:].bitcast(E4M3),
+                scales=z_plane[u, k][:],
+                in_=shared[(2 * u + k // 2) % SHARED][:].bitcast(BF16),
             )
 
+        def widen_resp():
+            nc.scalar.copy(out=resp_wide[:], in_=resp_rows[:])
+
         def turn_resp():
-            bank = psum.tile([P, P], BF16, name="for_scalar", bufs=SCALAR_BANKS)
-            nc.tensor.transpose(bank[:], resp_rows[:], ident_bf16[:])
+            bank = next_bank()
+            nc.tensor.transpose(bank[:, 0:P], resp_wide[:], ident[:])
             nc.scalar.copy(out=resp_col[:], in_=bank[:, 0 : F // P])
 
         def mix_matmul(u, k):
-            if (u, k) == (0, 0):
-                turn_resp()
-            bank = psum.tile([P, C], F32, name="for_scalar", bufs=SCALAR_BANKS)
+            bank = next_bank()
             bank_of["mix", u, k] = bank
             nc.tensor.matmul_mx(
                 out=bank[:],
-                lhsT=z_codes[u][:, P * k : P * (k + 1)].bitcast(E4M3),
-                lhsT_scale=z_plane[u][:, P * k : P * (k + 1)],
+                lhsT=z_codes[u, k - k % 2][:, P * (k % 2) : P * (k % 2 + 1)].bitcast(E4M3),
+                lhsT_scale=z_plane[u, k - k % 2][:, P * (k % 2) : P * (k % 2 + 1)],
                 rhs=m_codes[:].bitcast(E2M1),
                 rhs_scale=m_plane[:],
                 start=True,
@@ -312,81 +270,102 @@ def tile_orchestra_bleed_mix_t2_kernel(
             )
 
         def respond(u, k):
-            if u not in scaled:
-                scaled[u] = work.tile([P, 4, C], F32, align_bytes=64, name="scaled")
+            scaled[u, k] = work.tile([P, C], F32, align_bytes=64, name="scaled", bufs=4)
             b = 4 * (u % 2) + k
             nc.scalar.activation(
-                out=scaled[u][:, k, :], in_=bank_of["mix", u, k][:], func=COPY, scale=resp_col[:, b : b + 1]
+                out=scaled[u, k][:], in_=bank_of["mix", u, k][:], func=COPY, scale=resp_col[:, b : b + 1]
             )
 
-        def turn_back(u, m):
-            if on_gpsimd(u, m):
-                bank = psum.tile([P, 4, P], F32, name="for_scalar", bufs=SCALAR_BANKS)
-            else:
-                bank = psum.tile([P, 4, P], F32, name="for_vector", bufs=VECTOR_BANKS)
-            bank_of["back", u, m] = bank
-            for k in range(4):
-                nc.tensor.transpose(bank[:, k, :], scaled[u][:, k, P * m : P * (m + 1)], ident[:])
+        def turn_back(n, m):
+            u, k = n // 2, 2 * (n % 2)
+            bank = next_bank()
+            bank_of["back", n, m] = bank
+            for dm in range(2):
+                for dk in range(2):
+                    nc.tensor.transpose(
+                        bank[:, Q * dm + P * dk : Q * dm + P * (dk + 1)],
+                        scaled[u, k + dk][:, P * (m + dm) : P * (m + dm + 1)],
+                        ident[:],
+                    )
 
-        def store(u, m, result):
-            r, g = divmod(u, 2)
-            nc.sync.dma_start(out=out[P * m : P * (m + 1), r, g * W : (g + 1) * W], in_=result[:])
-            if u == 3 and 3 not in recs:
+        def add_record(engine, n, m, first, result):
+            r, bins = n // 4, slice(Q * (n % 4), Q * (n % 4 + 1))
+            result = result.rearrange("p (m f) -> p m f", m=2)
+            engine.tensor_tensor(
+                out=result, in0=first.rearrange("p (m f) -> p m f", m=2), in1=recs[r][:, m : m + 2, bins], op=ADD
+            )
+            nc.sync.dma_start(out=out.rearrange("(m c) r f -> c m r f", c=P)[:, m : m + 2, r, bins], in_=result)
+            if (n, m) == (3, 2):
                 load_rec(3)
 
-        def copy_out(u, m):
-            if on_gpsimd(u, m):
-                copied[u, m] = work.tile([P, W], F32, name="copied", bufs=3)
-                nc.scalar.copy(out=copied[u, m][:], in_=bank_of["back", u, m][:].rearrange("p k f -> p (k f)"))
-
-        def add_record_gpsimd(u, m):
-            if on_gpsimd(u, m):
-                r, g = divmod(u, 2)
+        def add_record_vector(n, m):
+            if not on_gpsimd(n, m):
                 result = work.tile([P, W], F32, name="result", bufs=RESULTS)
-                for f0 in range(0, W, W // 2):
-                    nc.gpsimd.tensor_tensor(
-                        out=result[:, f0 : f0 + W // 2],
-                        in0=copied[u, m][:, f0 : f0 + W // 2],
-                        in1=recs[r][:, m, g * W + f0 : g * W + f0 + W // 2],
-                        op=ADD,
-                    )
-                store(u, m, result)
+                add_record(nc.vector, n, m, bank_of["back", n, m][:], result[:])
 
-        def add_record(u, m):
-            if on_gpsimd(u, m):
-                return
-            r, g = divmod(u, 2)
-            result = work.tile([P, W], F32, name="result", bufs=RESULTS)
-            nc.vector.tensor_tensor(
-                out=result[:],
-                in0=bank_of["back", u, m][:].rearrange("p k f -> p (k f)"),
-                in1=recs[r][:, m, g * W : (g + 1) * W],
-                op=ADD,
-            )
-            store(u, m, result)
+        def copy_back(n, m):
+            if on_gpsimd(n, m):
+                copied[n] = work.tile([P, W], F32, name="copied")
+                nc.scalar.copy(out=copied[n][:], in_=bank_of["back", n, m][:])
 
-        stages = {
-            "interleave": interleave,
-            "quantise_x": lambda u, i: quantise_x(u),
-            "bleed_matmul": bleed_matmul,
-            "bleed": bleed,
-            "round_y": round_y,
-            "turn_y": turn_y,
-            "gather_y": gather_y,
-            "quantise_y": lambda u, i: quantise_y(u),
-            "leak_matmul": leak_matmul,
-            "leak": leak,
-            "quantise_z": lambda u, i: quantise_z(u),
-            "mix_matmul": mix_matmul,
-            "respond": respond,
-            "turn_back": turn_back,
-            "add_record": add_record,
-            "copy_out": copy_out,
-            "add_record_gpsimd": add_record_gpsimd,
-        }
-        last_lag = max(lag for stage, steps, lag in ROUND)
-        for h in range(HALF_FRAMES + last_lag):
-            for stage, steps, lag in ROUND:
-                if 0 <= h - lag < HALF_FRAMES:
-                    for i in steps:
-                        stages[stage](h - lag, i)
+        def add_record_gpsimd(n, m, quantised):
+            if on_gpsimd(n, m):
+                add_record(nc.gpsimd, n, m, copied[n][:], shared[quantised % SHARED][:])
+
+        def at(stage, n, *rest):
+            if 0 <= n < QUARTERS:
+                stage(n, *rest)
+
+        def pair(stage, n, *offsets):
+            if 0 <= n < QUARTERS:
+                for i in offsets:
+                    stage(n // 2, 2 * (n % 2) + i)
+
+        reorder_a()
+        interleave(0, 0, Q, "vector")
+        interleave(1, 0, Q, "scalar")
+        quantise_x(0)
+        quantise_x(1)
+        pair(bleed_matmul, 0, 0, 1)
+        interleave(2, 0, Q, "vector")
+        interleave(3, 0, Q, "scalar")
+        quantise_x(2)
+        quantise_x(3)
+        interleave(4, 0, Q, "gpsimd")
+        interleave(5, 0, Q, "gpsimd")
+        interleave(6, 0, Q, "gpsimd")
+        for n in range(QUARTERS + 9):
+            if n >= 5:
+                pair(bleed_matmul, n, 0, 1)
+            pair(leak_matmul, n - 6, 0, 1)
+            pair(mix_matmul, n - 7, 0, 1)
+            if n < 3:
+                pair(bleed_matmul, n + 1, 0, 1)
+            pair(bleed, n, 0, 1)
+            pair(round_y, n, 0)
+            pair(respond, n - 7, 0, 1)
+            if n == 6:
+                turn_resp()
+            pair(turn_y, n - 1, 0)
+            at(turn_back, n - 8, 0)
+            at(turn_back, n - 8, 2)
+            pair(leak, n - 6, 0, 1)
+            if n == 3:
+                quantise_x(4)
+                quantise_x(5)
+                pair(bleed_matmul, 4, 0, 1)
+                pair(quantise_y, 0, 0)
+            if n >= 3:
+                at(quantise_x, n + 3)
+                pair(quantise_y, n - 2, 0)
+            pair(quantise_z, n - 6, 0)
+            pair(gather_y, n - 1, 0)
+            at(copy_back, n - 8, 2)
+            if n >= 3:
+                at(interleave, n + 4, 0, GPSIMD_BINS, "gpsimd")
+                at(interleave, n + 4, GPSIMD_BINS, Q, "scalar")
+            if n == 5:
+                widen_resp()
+            at(add_record_gpsimd, n - 9, 2, n - 6)
+            at(add_record_vector, n - 8, 0)
+            at(add_record_vector, n - 8, 2)

@@ -25,9 +25,9 @@ Q = 256
 QUARTERS = 4 * T
 BANKS = 8
 RESULTS = 8
-SHARED = 6
-GPSIMD_QUARTERS = 8
-GPSIMD_BINS = 192
+SHARED = 8
+GPSIMD_QUARTERS = 13
+SPLITS = {6: 0, 7: 128}
 
 
 def tile_orchestra_bleed_mix_t2_kernel(
@@ -112,11 +112,13 @@ def tile_orchestra_bleed_mix_t2_kernel(
         for r in range(3):
             load_rec(r)
 
-        def reorder_a():
+        def reorder_a_codes():
             nc.vector.tensor_copy(
                 out=a_codes[:].bitcast(U16).rearrange("p (t m) -> p t m", t=4),
                 in_=a_arrived[:].bitcast(U16).rearrange("p (m t) -> p t m", t=4),
             )
+
+        def reorder_a_scales():
             nc.vector.tensor_copy(
                 out=a_plane[:].rearrange("p (t m) -> p t m", t=4),
                 in_=a_scales_arrived[:].rearrange("p (m t) -> p t m", t=4),
@@ -128,7 +130,7 @@ def tile_orchestra_bleed_mix_t2_kernel(
 
         def interleave(n, f0, f1, engine):
             if n not in grouped:
-                name, bufs = ("grouped_early", 4) if n < 6 else ("grouped", 1)
+                name, bufs = ("grouped_early", 4) if n < 6 or n in (7, 8) else ("grouped", 1)
                 grouped[n] = work.tile([P, Q, 4], BF16, align_bytes=64, name=name, bufs=bufs)
             out_ap = grouped[n][:, f0:f1, :]
             in_ap = raw[n // 4][:, :, Q * (n % 4) + f0 : Q * (n % 4) + f1]
@@ -184,7 +186,7 @@ def tile_orchestra_bleed_mix_t2_kernel(
             )
 
         def round_y(u, t):
-            y_bf16[u, t] = work.tile([P, 2 * W], BF16, align_bytes=64, name="y_bf16", bufs=3)
+            y_bf16[u, t] = work.tile([P, 2 * W], BF16, align_bytes=64, name="y_bf16", bufs=4)
             nc.scalar.copy(
                 out=y_bf16[u, t][:].rearrange("p (t h w e) -> p t h w e", t=2, h=2, e=2),
                 in_=y[u][:, t : t + 2, :].rearrange("p t (w h e) -> p t h w e", h=2, e=2),
@@ -198,7 +200,7 @@ def tile_orchestra_bleed_mix_t2_kernel(
                 nc.tensor.transpose(bank[:, P * j : P * (j + 1)], pairs, ident[:])
 
         def gather_y(u, t):
-            y_turned[u, t] = work.tile([P, 2 * S], BF16, align_bytes=64, name="y_turned", bufs=3)
+            y_turned[u, t] = work.tile([P, 2 * S], BF16, align_bytes=64, name="y_turned", bufs=4)
             nc.scalar.copy(
                 out=y_turned[u, t][:].bitcast(F32).rearrange("p (t j h) -> p t j h", t=2, h=2),
                 in_=bank_of["turn", u, t][:].rearrange("p (t h j) -> p t j h", t=2, h=2),
@@ -321,51 +323,80 @@ def tile_orchestra_bleed_mix_t2_kernel(
                 for i in offsets:
                     stage(n // 2, 2 * (n % 2) + i)
 
-        reorder_a()
+        reorder_a_codes()
         interleave(0, 0, Q, "vector")
         interleave(1, 0, Q, "scalar")
+        reorder_a_scales()
         quantise_x(0)
         quantise_x(1)
         pair(bleed_matmul, 0, 0, 1)
+        pair(bleed_matmul, 1, 0, 1)
         interleave(2, 0, Q, "vector")
         interleave(3, 0, Q, "scalar")
         quantise_x(2)
         quantise_x(3)
-        interleave(4, 0, Q, "gpsimd")
-        interleave(5, 0, Q, "gpsimd")
-        interleave(6, 0, Q, "gpsimd")
-        for n in range(QUARTERS + 9):
-            if n >= 5:
+        pair(bleed_matmul, 2, 0, 1)
+        pair(bleed_matmul, 3, 0, 1)
+        for n in range(4, 7):
+            interleave(n, 0, Q, "gpsimd")
+        for n in range(4):
+            pair(bleed, n, 0, 1)
+            pair(round_y, n, 0)
+            if n < 2:
+                pair(turn_y, n, 0)
+        quantise_x(4)
+        quantise_x(5)
+        interleave(7, 0, Q, "vector")
+        quantise_x(6)
+        quantise_x(7)
+        interleave(9, 0, Q, "gpsimd")
+        pair(bleed_matmul, 4, 0, 1)
+        pair(turn_y, 2, 0)
+        pair(turn_y, 3, 0)
+        pair(gather_y, 0, 0)
+        pair(gather_y, 1, 0)
+        widen_resp()
+        pair(gather_y, 2, 0)
+        pair(gather_y, 3, 0)
+        pair(bleed_matmul, 5, 0, 1)
+        pair(bleed, 4, 0, 1)
+        pair(quantise_y, 0, 0)
+        pair(quantise_y, 1, 0)
+        pair(round_y, 4, 0)
+        pair(bleed, 5, 0, 1)
+        pair(bleed_matmul, 6, 0, 1)
+        pair(quantise_y, 2, 0)
+        pair(quantise_y, 3, 0)
+        pair(round_y, 5, 0)
+        interleave(8, 0, Q, "scalar")
+        for n in range(6, QUARTERS + 9):
+            if n >= 7:
                 pair(bleed_matmul, n, 0, 1)
             pair(leak_matmul, n - 6, 0, 1)
             pair(mix_matmul, n - 7, 0, 1)
-            if n < 3:
-                pair(bleed_matmul, n + 1, 0, 1)
             pair(bleed, n, 0, 1)
+            if n == 6:
+                pair(turn_y, 4, 0)
+                turn_resp()
+                pair(gather_y, 4, 0)
             pair(round_y, n, 0)
             pair(respond, n - 7, 0, 1)
-            if n == 6:
-                turn_resp()
             pair(turn_y, n - 1, 0)
             at(turn_back, n - 8, 0)
             at(turn_back, n - 8, 2)
             pair(leak, n - 6, 0, 1)
-            if n == 3:
-                quantise_x(4)
-                quantise_x(5)
-                pair(bleed_matmul, 4, 0, 1)
-                pair(quantise_y, 0, 0)
-            if n >= 3:
-                at(quantise_x, n + 3)
-                pair(quantise_y, n - 2, 0)
+            if n == 6:
+                quantise_x(8)
+            at(quantise_x, n + 3)
+            pair(quantise_y, n - 2, 0)
             pair(quantise_z, n - 6, 0)
             pair(gather_y, n - 1, 0)
             at(copy_back, n - 8, 2)
-            if n >= 3:
-                at(interleave, n + 4, 0, GPSIMD_BINS, "gpsimd")
-                at(interleave, n + 4, GPSIMD_BINS, Q, "scalar")
-            if n == 5:
-                widen_resp()
-            at(add_record_gpsimd, n - 9, 2, n - 6)
+            split = SPLITS.get(n, Q)
+            if split > 0:
+                at(interleave, n + 4, 0, split, "gpsimd")
+            if split < Q:
+                at(interleave, n + 4, split, Q, "scalar")
             at(add_record_vector, n - 8, 0)
             at(add_record_vector, n - 8, 2)
+            at(add_record_gpsimd, n - 9, 2, n - 6)

@@ -27,7 +27,9 @@ BANKS = 8
 RESULTS = 8
 SHARED = 8
 GPSIMD_QUARTERS = 13
-SPLITS = {6: 0, 7: 128}
+SPLITS = {6: 128, 9: 192, 10: 192, 11: 192}
+BOTH = ()
+HALF_TURNED = (9, 11)
 
 
 def tile_orchestra_bleed_mix_t2_kernel(
@@ -51,6 +53,7 @@ def tile_orchestra_bleed_mix_t2_kernel(
         damp_col = keep.tile([P, 4], BF16, name="damp_col")
         resp_rows = keep.tile([P, P], BF16, align_bytes=64, name="resp_rows")
         resp_wide = keep.tile([P, P], F32, align_bytes=64, name="resp_wide")
+        resp_all = keep.tile([P, F], BF16, align_bytes=64, name="resp_all")
         resp_col = keep.tile([P, F // P], F32, name="resp_col")
         ident = keep.tile([P, P], F32, align_bytes=64, name="ident")
         raw = []
@@ -63,11 +66,14 @@ def tile_orchestra_bleed_mix_t2_kernel(
             shared_i = keep.tile([P, W], F32, align_bytes=64, name="shared%d" % i)
             shared.append(shared_i)
 
+        def turned_width(n):
+            return C // 2 if n in HALF_TURNED else C
+
         def as_int32(ap):
             return ap.bitcast(I32)
 
         def on_gpsimd(n, m):
-            return n < GPSIMD_QUARTERS and m == 2
+            return n < GPSIMD_QUARTERS if m == 2 else n in BOTH
 
         nc.vector.memset(as_int32(a_scales_arrived[:]), 0)
         nc.vector.memset(ident[:], 0.0)
@@ -111,6 +117,7 @@ def tile_orchestra_bleed_mix_t2_kernel(
         load_x(3, 0, F)
         for r in range(3):
             load_rec(r)
+        nc.sync.dma_start(out=resp_all[:], in_=resp.partition_broadcast(P))
 
         def reorder_a_codes():
             nc.vector.tensor_copy(
@@ -259,26 +266,58 @@ def tile_orchestra_bleed_mix_t2_kernel(
             nc.scalar.copy(out=resp_col[:], in_=bank[:, 0 : F // P])
 
         def mix_matmul(u, k):
-            bank = next_bank()
-            bank_of["mix", u, k] = bank
+            width = turned_width(2 * u + k // 2)
+            if k % 2 * width % W == 0:
+                bank_of["mix bank"] = next_bank()
+            bank_of["mix", u, k] = bank_of["mix bank"][:, k % 2 * width % W : k % 2 * width % W + width]
             nc.tensor.matmul_mx(
-                out=bank[:],
+                out=bank_of["mix", u, k],
                 lhsT=z_codes[u, k - k % 2][:, P * (k % 2) : P * (k % 2 + 1)].bitcast(E4M3),
                 lhsT_scale=z_plane[u, k - k % 2][:, P * (k % 2) : P * (k % 2 + 1)],
-                rhs=m_codes[:].bitcast(E2M1),
-                rhs_scale=m_plane[:],
+                rhs=m_codes[:, 0 : 2 * width].bitcast(E2M1),
+                rhs_scale=m_plane[:, 0:width],
                 start=True,
                 stop=True,
             )
 
+        def mix_by_microphones(u, k):
+            if turned_width(2 * u + k // 2) == C:
+                return
+            bank = next_bank()
+            bank_of["microphones", u, k] = bank
+            for dm in range(2):
+                nc.tensor.matmul_mx(
+                    out=bank[:, Q * dm : Q * (dm + 1)],
+                    lhsT=m_codes[:, 2 * P * (2 + dm) : 2 * P * (3 + dm)].bitcast(E2M1),
+                    lhsT_scale=m_plane[:, P * (2 + dm) : P * (3 + dm)],
+                    rhs=z_codes[u, k][:].bitcast(E4M3),
+                    rhs_scale=z_plane[u, k][:],
+                    start=True,
+                    stop=True,
+                )
+
+        def respond_by_microphones(u, k):
+            n = 2 * u + k // 2
+            if turned_width(n) == C:
+                return
+            copied[n, 2] = work.tile([P, W], F32, name="copied", bufs=6)
+            nc.vector.tensor_tensor(
+                out=copied[n, 2][:].rearrange("p (m f) -> p m f", m=2),
+                in0=bank_of["microphones", u, k][:].rearrange("p (m f) -> p m f", m=2),
+                in1=resp_all[:, Q * (n % 4) : Q * (n % 4 + 1)].unsqueeze(1).to_broadcast([P, 2, Q]),
+                op=MULT,
+            )
+
         def respond(u, k):
-            scaled[u, k] = work.tile([P, C], F32, align_bytes=64, name="scaled", bufs=4)
+            scaled[u, k] = work.tile([P, turned_width(2 * u + k // 2)], F32, align_bytes=64, name="scaled", bufs=4)
             b = 4 * (u % 2) + k
             nc.scalar.activation(
-                out=scaled[u, k][:], in_=bank_of["mix", u, k][:], func=COPY, scale=resp_col[:, b : b + 1]
+                out=scaled[u, k][:], in_=bank_of["mix", u, k], func=COPY, scale=resp_col[:, b : b + 1]
             )
 
         def turn_back(n, m):
+            if P * m >= turned_width(n):
+                return
             u, k = n // 2, 2 * (n % 2)
             bank = next_bank()
             bank_of["back", n, m] = bank
@@ -306,13 +345,13 @@ def tile_orchestra_bleed_mix_t2_kernel(
                 add_record(nc.vector, n, m, bank_of["back", n, m][:], result[:])
 
         def copy_back(n, m):
-            if on_gpsimd(n, m):
-                copied[n] = work.tile([P, W], F32, name="copied")
-                nc.scalar.copy(out=copied[n][:], in_=bank_of["back", n, m][:])
+            if on_gpsimd(n, m) and P * m < turned_width(n):
+                copied[n, m] = work.tile([P, W], F32, name="copied", bufs=6)
+                nc.scalar.copy(out=copied[n, m][:], in_=bank_of["back", n, m][:])
 
         def add_record_gpsimd(n, m, quantised):
             if on_gpsimd(n, m):
-                add_record(nc.gpsimd, n, m, copied[n][:], shared[quantised % SHARED][:])
+                add_record(nc.gpsimd, n, m, copied[n, m][:], shared[quantised % SHARED][:] if m == 2 else copied[n, m][:])
 
         def at(stage, n, *rest):
             if 0 <= n < QUARTERS:
@@ -325,7 +364,8 @@ def tile_orchestra_bleed_mix_t2_kernel(
 
         reorder_a_codes()
         interleave(0, 0, Q, "vector")
-        interleave(1, 0, Q, "scalar")
+        interleave(1, 0, P, "vector")
+        interleave(1, P, Q, "scalar")
         reorder_a_scales()
         quantise_x(0)
         quantise_x(1)
@@ -334,13 +374,14 @@ def tile_orchestra_bleed_mix_t2_kernel(
         interleave(2, 0, Q, "vector")
         interleave(3, 0, Q, "scalar")
         quantise_x(2)
+        pair(bleed, 0, 0)
         quantise_x(3)
         pair(bleed_matmul, 2, 0, 1)
         pair(bleed_matmul, 3, 0, 1)
         for n in range(4, 7):
             interleave(n, 0, Q, "gpsimd")
         for n in range(4):
-            pair(bleed, n, 0, 1)
+            pair(bleed, n, *((1,) if n == 0 else (0, 1)))
             pair(round_y, n, 0)
             if n < 2:
                 pair(turn_y, n, 0)
@@ -374,6 +415,7 @@ def tile_orchestra_bleed_mix_t2_kernel(
                 pair(bleed_matmul, n, 0, 1)
             pair(leak_matmul, n - 6, 0, 1)
             pair(mix_matmul, n - 7, 0, 1)
+            pair(mix_by_microphones, n - 7, 0)
             pair(bleed, n, 0, 1)
             if n == 6:
                 pair(turn_y, 4, 0)
@@ -385,12 +427,14 @@ def tile_orchestra_bleed_mix_t2_kernel(
             at(turn_back, n - 8, 0)
             at(turn_back, n - 8, 2)
             pair(leak, n - 6, 0, 1)
+            pair(respond_by_microphones, n - 7, 0)
             if n == 6:
                 quantise_x(8)
             at(quantise_x, n + 3)
             pair(quantise_y, n - 2, 0)
             pair(quantise_z, n - 6, 0)
             pair(gather_y, n - 1, 0)
+            at(copy_back, n - 8, 0)
             at(copy_back, n - 8, 2)
             split = SPLITS.get(n, Q)
             if split > 0:
@@ -400,3 +444,4 @@ def tile_orchestra_bleed_mix_t2_kernel(
             at(add_record_vector, n - 8, 0)
             at(add_record_vector, n - 8, 2)
             at(add_record_gpsimd, n - 9, 2, n - 6)
+            at(add_record_gpsimd, n - 9, 0, n - 6)

@@ -50,7 +50,8 @@ def tile_orchestra_bleed_mix_t2_kernel(
         l_plane = keep.tile([P, 2, F], U8, align_bytes=64, name="l_plane")
         m_codes = keep.tile([P, 2 * C], U8, align_bytes=64, name="m_codes")
         m_plane = keep.tile([P, C], U8, align_bytes=64, name="m_plane")
-        damp_col = keep.tile([P, 4], BF16, name="damp_col")
+        damp_arrived = keep.tile([P, 4], BF16, name="damp_arrived")
+        damp_col = keep.tile([P, 4], F32, name="damp_col")
         resp_rows = keep.tile([P, P], BF16, align_bytes=64, name="resp_rows")
         resp_wide = keep.tile([P, P], F32, align_bytes=64, name="resp_wide")
         resp_all = keep.tile([P, F], BF16, align_bytes=64, name="resp_all")
@@ -99,7 +100,7 @@ def tile_orchestra_bleed_mix_t2_kernel(
                 in_=as_int32(a_scales[0, 4 * q : 4 * q + 4, :]),
             )
         load_x(0, W, F)
-        nc.sync.dma_start(out=damp_col[:], in_=damp.rearrange("(p t) -> p t", t=4))
+        nc.sync.dma_start(out=damp_arrived[:], in_=damp.rearrange("(p t) -> p t", t=4))
         load_x(1, 0, F)
         nc.sync.dma_start(out=as_int32(l_codes[:]), in_=as_int32(l_words.rearrange("g p n -> p g n")))
         for q in range(4):
@@ -242,9 +243,9 @@ def tile_orchestra_bleed_mix_t2_kernel(
         def leak(u, k):
             half = shared[(2 * u + k // 2) % SHARED][:, Q * (k % 2) : Q * (k % 2 + 1)].bitcast(BF16)
             nc.vector.tensor_tensor(
-                out=half.rearrange("p (c i t) -> p c t i", i=2, t=4),
-                in0=bank_of["leak", u, k][:].rearrange("p (t c i) -> p c t i", t=4, i=2),
-                in1=y[u][:, :, P * k : P * (k + 1)].rearrange("p t (c i) -> p c t i", i=2),
+                out=half.rearrange("p (c i t) -> p c t i", i=4, t=4),
+                in0=bank_of["leak", u, k][:].rearrange("p (t c i) -> p c t i", t=4, i=4),
+                in1=y[u][:, :, P * k : P * (k + 1)].rearrange("p t (c i) -> p c t i", i=4),
                 op=ADD,
             )
 
@@ -373,6 +374,7 @@ def tile_orchestra_bleed_mix_t2_kernel(
         pair(bleed_matmul, 1, 0, 1)
         interleave(2, 0, Q, "vector")
         interleave(3, 0, Q, "scalar")
+        nc.vector.tensor_copy(out=damp_col[:], in_=damp_arrived[:])
         quantise_x(2)
         pair(bleed, 0, 0)
         quantise_x(3)

@@ -29,6 +29,7 @@ SHARED = 8
 GPSIMD_QUARTERS = 13
 SPLITS = {6: 128, 9: 192, 10: 192, 11: 192}
 BOTH = ()
+STAGING = {0: 0, 1: 1, 2: 2, 3: 3, 4: 3, 5: 0, 7: 1, 8: 2}
 HALF_TURNED = (9, 11)
 
 
@@ -70,6 +71,11 @@ def tile_orchestra_bleed_mix_t2_kernel(
         def turned_width(n):
             return C // 2 if n in HALF_TURNED else C
 
+        staged = []
+        for i in range(5):
+            staged_i = keep.tile([P, Q, 4], BF16, align_bytes=64, name="staged%d" % i)
+            staged.append(staged_i)
+
         def as_int32(ap):
             return ap.bitcast(I32)
 
@@ -101,15 +107,16 @@ def tile_orchestra_bleed_mix_t2_kernel(
             )
         load_x(0, W, F)
         nc.sync.dma_start(out=damp_arrived[:], in_=damp.rearrange("(p t) -> p t", t=4))
-        load_x(1, 0, F)
+        load_x(1, 0, W)
+        load_x(1, W, F)
+        load_x(2, 0, F)
+        nc.sync.dma_start(out=resp_rows[0 : F // P, :], in_=resp.rearrange("(b q) -> b q", q=P))
         nc.sync.dma_start(out=as_int32(l_codes[:]), in_=as_int32(l_words.rearrange("g p n -> p g n")))
         for q in range(4):
             nc.sync.dma_start(
                 out=as_int32(l_plane[32 * q : 32 * q + 4, :, :]),
                 in_=as_int32(l_scales[:, 4 * q : 4 * q + 4, :].rearrange("g q n -> q g n")),
             )
-        load_x(2, 0, F)
-        nc.sync.dma_start(out=resp_rows[0 : F // P, :], in_=resp.rearrange("(b q) -> b q", q=P))
         nc.sync.dma_start(out=as_int32(m_codes[:]), in_=as_int32(m_words[0]))
         for q in range(4):
             nc.sync.dma_start(
@@ -138,8 +145,7 @@ def tile_orchestra_bleed_mix_t2_kernel(
 
         def interleave(n, f0, f1, engine):
             if n not in grouped:
-                name, bufs = ("grouped_early", 4) if n < 6 or n in (7, 8) else ("grouped", 1)
-                grouped[n] = work.tile([P, Q, 4], BF16, align_bytes=64, name=name, bufs=bufs)
+                grouped[n] = staged[STAGING.get(n, 4)]
             out_ap = grouped[n][:, f0:f1, :]
             in_ap = raw[n // 4][:, :, Q * (n % 4) + f0 : Q * (n % 4) + f1]
             if engine == "gpsimd":
@@ -341,7 +347,15 @@ def tile_orchestra_bleed_mix_t2_kernel(
                 load_rec(3)
 
         def add_record_vector(n, m):
-            if not on_gpsimd(n, m):
+            if (n, m) == (QUARTERS - 1, 2):
+                for dm in range(2):
+                    result = work.tile([P, Q], F32, name="last")
+                    r, bins = n // 4, slice(Q * (n % 4), Q * (n % 4 + 1))
+                    nc.vector.tensor_tensor(
+                        out=result[:], in0=bank_of["back", n, m][:, Q * dm : Q * (dm + 1)], in1=recs[r][:, m + dm, bins], op=ADD
+                    )
+                    nc.sync.dma_start(out=out[P * (m + dm) : P * (m + dm + 1), r, bins], in_=result[:])
+            elif not on_gpsimd(n, m):
                 result = work.tile([P, W], F32, name="result", bufs=RESULTS)
                 add_record(nc.vector, n, m, bank_of["back", n, m][:], result[:])
 
@@ -376,14 +390,13 @@ def tile_orchestra_bleed_mix_t2_kernel(
         interleave(3, 0, Q, "scalar")
         nc.vector.tensor_copy(out=damp_col[:], in_=damp_arrived[:])
         quantise_x(2)
-        pair(bleed, 0, 0)
         quantise_x(3)
         pair(bleed_matmul, 2, 0, 1)
         pair(bleed_matmul, 3, 0, 1)
         for n in range(4, 7):
             interleave(n, 0, Q, "gpsimd")
         for n in range(4):
-            pair(bleed, n, *((1,) if n == 0 else (0, 1)))
+            pair(bleed, n, 0, 1)
             pair(round_y, n, 0)
             if n < 2:
                 pair(turn_y, n, 0)

@@ -26,11 +26,11 @@ QUARTERS = 4 * T
 BANKS = 8
 RESULTS = 8
 SHARED = 8
-GPSIMD_QUARTERS = 13
+GPSIMD_QUARTERS = 12
 SPLITS = {6: 128, 9: 192, 10: 192, 11: 192}
 BOTH = ()
 STAGING = {0: 0, 1: 1, 2: 2, 3: 3, 4: 3, 5: 0, 7: 1, 8: 2}
-HALF_TURNED = (9, 11)
+HALF_TURNED = (7, 9, 11)
 
 
 def tile_orchestra_bleed_mix_t2_kernel(
@@ -58,10 +58,7 @@ def tile_orchestra_bleed_mix_t2_kernel(
         resp_all = keep.tile([P, F], BF16, align_bytes=64, name="resp_all")
         resp_col = keep.tile([P, F // P], F32, name="resp_col")
         ident = keep.tile([P, P], F32, align_bytes=64, name="ident")
-        raw = []
-        for r in range(T):
-            raw_r = keep.tile([P, 4, F], BF16, align_bytes=64, name="raw%d" % r)
-            raw.append(raw_r)
+        raw = {}
 
         shared = []
         for i in range(SHARED):
@@ -90,7 +87,10 @@ def tile_orchestra_bleed_mix_t2_kernel(
         make_identity(nc, ident[:], nomemset=True)
 
         def load_x(r, f0, f1, queue=nc.sync):
-            queue.dma_start(out=raw[r][:, :, f0:f1], in_=x.rearrange("(p t) r f -> p t r f", t=4)[:, :, r, f0:f1])
+            loaded = keep.tile([P, 4, f1 - f0], BF16, align_bytes=64, name="raw%d_%d" % (r, f0))
+            queue.dma_start(out=loaded[:], in_=x.rearrange("(p t) r f -> p t r f", t=4)[:, :, r, f0:f1])
+            for f in range(f0, f1, W):
+                raw[2 * r + f // W] = loaded[:, :, f - f0 : f - f0 + W]
 
         recs = {}
 
@@ -147,7 +147,7 @@ def tile_orchestra_bleed_mix_t2_kernel(
             if n not in grouped:
                 grouped[n] = staged[STAGING.get(n, 4)]
             out_ap = grouped[n][:, f0:f1, :]
-            in_ap = raw[n // 4][:, :, Q * (n % 4) + f0 : Q * (n % 4) + f1]
+            in_ap = raw[n // 2][:, :, Q * (n % 2) + f0 : Q * (n % 2) + f1]
             if engine == "gpsimd":
                 nc.gpsimd.tensor_scalar(
                     out=out_ap, in0=in_ap.rearrange("p t f -> p f t"), scalar1=1.0, scalar2=0.0, op0=MULT, op1=ADD
@@ -187,14 +187,13 @@ def tile_orchestra_bleed_mix_t2_kernel(
             )
 
         def bleed(u, t):
-            r, g = divmod(u, 2)
             if u not in y:
                 y[u] = work.tile([P, 4, W], F32, align_bytes=64, name="y", bufs=5)
             nc.vector.scalar_tensor_tensor(
                 out=y[u][:, t, :],
                 in0=bank_of["bleed", u, t][:],
                 scalar=damp_col[:, t : t + 1],
-                in1=raw[r][:, t, g * W : (g + 1) * W],
+                in1=raw[u][:, t, :],
                 op0=MULT,
                 op1=ADD,
             )
@@ -258,11 +257,14 @@ def tile_orchestra_bleed_mix_t2_kernel(
         def quantise_z(u, k):
             z_codes[u, k] = work.tile([P, 2 * P], U32, align_bytes=64, name="z_codes", bufs=3)
             z_plane[u, k] = work.tile([P, 2 * P], U8, align_bytes=64, name="z_plane", bufs=3)
-            nc.vector.quantize_mx(
-                out=z_codes[u, k][:].bitcast(E4M3),
-                scales=z_plane[u, k][:],
-                in_=shared[(2 * u + k // 2) % SHARED][:].bitcast(BF16),
-            )
+            n = 2 * u + k // 2
+            width = P if n == QUARTERS - 1 else Q
+            for f0 in range(0, Q, width):
+                nc.vector.quantize_mx(
+                    out=z_codes[u, k][:, f0 : f0 + width].bitcast(E4M3),
+                    scales=z_plane[u, k][:, f0 : f0 + width],
+                    in_=shared[n % SHARED][:, 2 * f0 : 2 * (f0 + width)].bitcast(BF16),
+                )
 
         def widen_resp():
             nc.scalar.copy(out=resp_wide[:], in_=resp_rows[:])
@@ -388,8 +390,8 @@ def tile_orchestra_bleed_mix_t2_kernel(
         pair(bleed_matmul, 1, 0, 1)
         interleave(2, 0, Q, "vector")
         interleave(3, 0, Q, "scalar")
-        nc.vector.tensor_copy(out=damp_col[:], in_=damp_arrived[:])
         quantise_x(2)
+        nc.vector.tensor_copy(out=damp_col[:], in_=damp_arrived[:])
         quantise_x(3)
         pair(bleed_matmul, 2, 0, 1)
         pair(bleed_matmul, 3, 0, 1)
@@ -445,8 +447,8 @@ def tile_orchestra_bleed_mix_t2_kernel(
             pair(respond_by_microphones, n - 7, 0)
             if n == 6:
                 quantise_x(8)
-            at(quantise_x, n + 3)
             pair(quantise_y, n - 2, 0)
+            at(quantise_x, n + 3)
             pair(quantise_z, n - 6, 0)
             pair(gather_y, n - 1, 0)
             at(copy_back, n - 8, 0)

@@ -18,19 +18,22 @@ COPY = mybir.ActivationFunctionType.Copy
 S, T, F, C = 512, 4, 1024, 512
 P = 128
 W = 512
+Q = 256
 HALF_FRAMES = 2 * T
+QUARTERS = 4 * T
 FLOPS = 2 * (2 * S * S * T * F + S * T * F * F)
 
-Q = 256
-QUARTERS = 4 * T
 BANKS = 8
 RESULTS = 8
-SHARED = 8
+
+LEAK_LAG = 6
+MIX_LAG = LEAK_LAG + 1
+BACK_LAG = LEAK_LAG + 2
+X_LEAD = 3
+
 GPSIMD_QUARTERS = 12
-SPLITS = {6: 128, 9: 192, 10: 192, 11: 192}
-BOTH = ()
-STAGING = {0: 0, 1: 1, 2: 2, 3: 3, 4: 3, 5: 0, 7: 1, 8: 2}
-HALF_TURNED = (7, 9, 11)
+FIRST_HALF_TURNED = 7
+GPSIMD_BINS = 192
 
 
 def tile_orchestra_bleed_mix_t2_kernel(
@@ -58,26 +61,29 @@ def tile_orchestra_bleed_mix_t2_kernel(
         resp_all = keep.tile([P, F], BF16, align_bytes=64, name="resp_all")
         resp_col = keep.tile([P, F // P], F32, name="resp_col")
         ident = keep.tile([P, P], F32, align_bytes=64, name="ident")
-        raw = {}
-
-        shared = []
-        for i in range(SHARED):
-            shared_i = keep.tile([P, W], F32, align_bytes=64, name="shared%d" % i)
-            shared.append(shared_i)
-
-        def turned_width(n):
-            return C // 2 if n in HALF_TURNED else C
-
+        z_tiles = []
+        for i in range(RESULTS):
+            z_tile = keep.tile([P, W], F32, align_bytes=64, name="z%d" % i)
+            z_tiles.append(z_tile)
         staged = []
         for i in range(5):
-            staged_i = keep.tile([P, Q, 4], BF16, align_bytes=64, name="staged%d" % i)
-            staged.append(staged_i)
+            staged_tile = keep.tile([P, 4 * Q], BF16, align_bytes=64, name="staged%d" % i)
+            staged.append(staged_tile)
+
+        def grouped(n):
+            if n < 4:
+                return staged[n]
+            return staged[{4: 3, 5: 0, 6: 0, 7: 1, 8: 2}.get(n, 4)]
+
+        def turned_width(n):
+            half = FIRST_HALF_TURNED <= n < GPSIMD_QUARTERS and (n - FIRST_HALF_TURNED) % 2 == 0
+            return C // 2 if half else C
+
+        def on_gpsimd(n, m):
+            return m == 2 and n < GPSIMD_QUARTERS
 
         def as_int32(ap):
             return ap.bitcast(I32)
-
-        def on_gpsimd(n, m):
-            return n < GPSIMD_QUARTERS if m == 2 else n in BOTH
 
         nc.vector.memset(as_int32(a_scales_arrived[:]), 0)
         nc.vector.memset(ident[:], 0.0)
@@ -86,30 +92,31 @@ def tile_orchestra_bleed_mix_t2_kernel(
         nc.vector.memset(resp_rows[:], 0.0)
         make_identity(nc, ident[:], nomemset=True)
 
-        def load_x(r, f0, f1, queue=nc.sync):
-            loaded = keep.tile([P, 4, f1 - f0], BF16, align_bytes=64, name="raw%d_%d" % (r, f0))
-            queue.dma_start(out=loaded[:], in_=x.rearrange("(p t) r f -> p t r f", t=4)[:, :, r, f0:f1])
-            for f in range(f0, f1, W):
-                raw[2 * r + f // W] = loaded[:, :, f - f0 : f - f0 + W]
+        raw, recs = {}, {}
 
-        recs = {}
+        def load_x(u, halves, queue=nc.sync):
+            loaded = keep.tile([P, 4, halves * W], BF16, align_bytes=64, name="raw%d" % u)
+            bins = slice(W * (u % 2), W * (u % 2 + halves))
+            queue.dma_start(out=loaded[:], in_=x.rearrange("(p t) r f -> p t r f", t=4)[:, :, u // 2, bins])
+            for g in range(halves):
+                raw[u + g] = loaded[:, :, W * g : W * (g + 1)]
 
         def load_rec(r):
             recs[r] = work.tile([P, C // P, F], BF16, align_bytes=64, name="rec", bufs=3)
             nc.sync.dma_start(out=recs[r][:], in_=rec.rearrange("(m c) r f -> c m r f", c=P)[:, :, r, :])
 
-        load_x(0, 0, W, nc.scalar)
+        load_x(0, 1, nc.scalar)
         nc.sync.dma_start(out=as_int32(a_arrived[:]), in_=as_int32(a_words[0]))
         for q in range(4):
             nc.sync.dma_start(
                 out=as_int32(a_scales_arrived[32 * q : 32 * q + 4, :]),
                 in_=as_int32(a_scales[0, 4 * q : 4 * q + 4, :]),
             )
-        load_x(0, W, F)
+        load_x(1, 1)
         nc.sync.dma_start(out=damp_arrived[:], in_=damp.rearrange("(p t) -> p t", t=4))
-        load_x(1, 0, W)
-        load_x(1, W, F)
-        load_x(2, 0, F)
+        load_x(2, 1)
+        load_x(3, 1)
+        load_x(4, 2)
         nc.sync.dma_start(out=resp_rows[0 : F // P, :], in_=resp.rearrange("(b q) -> b q", q=P))
         nc.sync.dma_start(out=as_int32(l_codes[:]), in_=as_int32(l_words.rearrange("g p n -> p g n")))
         for q in range(4):
@@ -122,7 +129,7 @@ def tile_orchestra_bleed_mix_t2_kernel(
             nc.sync.dma_start(
                 out=as_int32(m_plane[32 * q : 32 * q + 4, :]), in_=as_int32(m_scales[0, 4 * q : 4 * q + 4, :])
             )
-        load_x(3, 0, F)
+        load_x(6, 2)
         for r in range(3):
             load_rec(r)
         nc.sync.dma_start(out=resp_all[:], in_=resp.partition_broadcast(P))
@@ -139,14 +146,14 @@ def tile_orchestra_bleed_mix_t2_kernel(
                 in_=a_scales_arrived[:].rearrange("p (m t) -> p t m", t=4),
             )
 
-        grouped, x_codes, x_plane = {}, {}, {}
-        y, y_bf16, y_turned, y_codes, y_plane = {}, {}, {}, {}, {}
-        z_codes, z_plane, scaled, copied, bank_of = {}, {}, {}, {}, {}
+        x_codes, x_plane, y, y_bf16, y_turned, y_codes, y_plane = {}, {}, {}, {}, {}, {}, {}
+        z_codes, z_plane, scaled, unrecorded, bank_of = {}, {}, {}, {}, {}
+
+        def next_bank():
+            return psum.tile([P, W], F32, name="bank", bufs=BANKS)
 
         def interleave(n, f0, f1, engine):
-            if n not in grouped:
-                grouped[n] = staged[STAGING.get(n, 4)]
-            out_ap = grouped[n][:, f0:f1, :]
+            out_ap = grouped(n)[:, 4 * f0 : 4 * f1].rearrange("p (f t) -> p f t", t=4)
             in_ap = raw[n // 2][:, :, Q * (n % 2) + f0 : Q * (n % 2) + f1]
             if engine == "gpsimd":
                 nc.gpsimd.tensor_scalar(
@@ -161,109 +168,116 @@ def tile_orchestra_bleed_mix_t2_kernel(
 
         def quantise_x(n):
             u, j = divmod(n, 2)
-            if u not in x_codes:
+            if j == 0:
                 x_codes[u] = work.tile([P, W], U32, align_bytes=64, name="x_codes", bufs=3)
                 x_plane[u] = work.tile([P, W], U8, align_bytes=64, name="x_plane", bufs=3)
             nc.vector.quantize_mx(
                 out=x_codes[u][:, Q * j : Q * (j + 1)].bitcast(E4M3),
                 scales=x_plane[u][:, Q * j : Q * (j + 1)],
-                in_=grouped[n][:].rearrange("p f t -> p (f t)"),
+                in_=grouped(n)[:],
             )
 
-        def next_bank():
-            return psum.tile([P, W], F32, name="bank", bufs=BANKS)
+        def bleed_matmuls(n):
+            u, j = divmod(n, 2)
+            for t in (2 * j, 2 * j + 1):
+                bank_of["bleed", u, t] = next_bank()
+                nc.tensor.matmul_mx(
+                    out=bank_of["bleed", u, t][:],
+                    lhsT=a_codes[:, 2 * P * t : 2 * P * (t + 1)].bitcast(E2M1),
+                    lhsT_scale=a_plane[:, P * t : P * (t + 1)],
+                    rhs=x_codes[u][:].bitcast(E4M3),
+                    rhs_scale=x_plane[u][:],
+                    start=True,
+                    stop=True,
+                )
 
-        def bleed_matmul(u, t):
-            bank = next_bank()
-            bank_of["bleed", u, t] = bank
-            nc.tensor.matmul_mx(
-                out=bank[:],
-                lhsT=a_codes[:, 2 * P * t : 2 * P * (t + 1)].bitcast(E2M1),
-                lhsT_scale=a_plane[:, P * t : P * (t + 1)],
-                rhs=x_codes[u][:].bitcast(E4M3),
-                rhs_scale=x_plane[u][:],
-                start=True,
-                stop=True,
-            )
-
-        def bleed(u, t):
-            if u not in y:
+        def bleed(n):
+            u, j = divmod(n, 2)
+            if j == 0:
                 y[u] = work.tile([P, 4, W], F32, align_bytes=64, name="y", bufs=5)
-            nc.vector.scalar_tensor_tensor(
-                out=y[u][:, t, :],
-                in0=bank_of["bleed", u, t][:],
-                scalar=damp_col[:, t : t + 1],
-                in1=raw[u][:, t, :],
-                op0=MULT,
-                op1=ADD,
-            )
+            for t in (2 * j, 2 * j + 1):
+                nc.vector.scalar_tensor_tensor(
+                    out=y[u][:, t, :],
+                    in0=bank_of["bleed", u, t][:],
+                    scalar=damp_col[:, t : t + 1],
+                    in1=raw[u][:, t, :],
+                    op0=MULT,
+                    op1=ADD,
+                )
 
-        def round_y(u, t):
-            y_bf16[u, t] = work.tile([P, 2 * W], BF16, align_bytes=64, name="y_bf16", bufs=4)
+        def round_y(n):
+            u, j = divmod(n, 2)
+            y_bf16[n] = work.tile([P, 2 * W], BF16, align_bytes=64, name="y_bf16", bufs=4)
             nc.scalar.copy(
-                out=y_bf16[u, t][:].rearrange("p (t h w e) -> p t h w e", t=2, h=2, e=2),
-                in_=y[u][:, t : t + 2, :].rearrange("p t (w h e) -> p t h w e", h=2, e=2),
+                out=y_bf16[n][:].rearrange("p (t h w e) -> p t h w e", t=2, h=2, e=2),
+                in_=y[u][:, 2 * j : 2 * j + 2, :].rearrange("p t (w h e) -> p t h w e", h=2, e=2),
             )
 
-        def turn_y(u, t):
-            bank = next_bank()
-            bank_of["turn", u, t] = bank
-            for j in range(4):
-                pairs = y_bf16[u, t][:, 2 * P * j : 2 * P * (j + 1)].bitcast(F32)
-                nc.tensor.transpose(bank[:, P * j : P * (j + 1)], pairs, ident[:])
+        def turn_y(n):
+            bank_of["turn", n] = next_bank()
+            for i in range(4):
+                pairs = y_bf16[n][:, 2 * P * i : 2 * P * (i + 1)].bitcast(F32)
+                nc.tensor.transpose(bank_of["turn", n][:, P * i : P * (i + 1)], pairs, ident[:])
 
-        def gather_y(u, t):
-            y_turned[u, t] = work.tile([P, 2 * S], BF16, align_bytes=64, name="y_turned", bufs=4)
+        def gather_y(n):
+            if n == 3:
+                y_turned[n] = staged[4]
+            else:
+                y_turned[n] = work.tile([P, 2 * S], BF16, align_bytes=64, name="y_turned", bufs=4)
             nc.scalar.copy(
-                out=y_turned[u, t][:].bitcast(F32).rearrange("p (t j h) -> p t j h", t=2, h=2),
-                in_=bank_of["turn", u, t][:].rearrange("p (t h j) -> p t j h", t=2, h=2),
+                out=y_turned[n][:].bitcast(F32).rearrange("w (t p h) -> w t p h", t=2, h=2),
+                in_=bank_of["turn", n][:].rearrange("w (t h p) -> w t p h", t=2, h=2),
             )
 
-        def quantise_y(u, t):
-            if u not in y_codes:
+        def quantise_y(n):
+            u, j = divmod(n, 2)
+            if j == 0:
                 y_codes[u] = work.tile([P, S], U32, align_bytes=64, name="y_codes", bufs=4)
                 y_plane[u] = work.tile([P, S], U8, align_bytes=64, name="y_plane", bufs=4)
             nc.vector.quantize_mx(
-                out=y_codes[u][:, P * t : P * (t + 2)].bitcast(E4M3),
-                scales=y_plane[u][:, P * t : P * (t + 2)],
-                in_=y_turned[u, t][:],
+                out=y_codes[u][:, Q * j : Q * (j + 1)].bitcast(E4M3),
+                scales=y_plane[u][:, Q * j : Q * (j + 1)],
+                in_=y_turned[n][:],
             )
 
-        def leak_matmul(u, k):
-            r, b = u // 2, 4 * (u % 2) + k
-            bank = next_bank()
-            bank_of["leak", u, k] = bank
-            for t in range(4):
-                for g in range(2):
-                    nc.tensor.matmul_mx(
-                        out=bank[:, P * t : P * (t + 1)],
-                        lhsT=y_codes[2 * r + g][:, P * t : P * (t + 1)].bitcast(E4M3),
-                        lhsT_scale=y_plane[2 * r + g][:, P * t : P * (t + 1)],
-                        rhs=l_codes[:, g, 2 * P * b : 2 * P * (b + 1)].bitcast(E2M1),
-                        rhs_scale=l_plane[:, g, P * b : P * (b + 1)],
-                        start=(g == 0),
-                        stop=(g == 1),
-                    )
+        def leak_matmuls(n):
+            r = n // 4
+            for k in range(2):
+                b = 2 * (n % 4) + k
+                bank_of["leak", n, k] = next_bank()
+                for t in range(4):
+                    for g in range(2):
+                        nc.tensor.matmul_mx(
+                            out=bank_of["leak", n, k][:, P * t : P * (t + 1)],
+                            lhsT=y_codes[2 * r + g][:, P * t : P * (t + 1)].bitcast(E4M3),
+                            lhsT_scale=y_plane[2 * r + g][:, P * t : P * (t + 1)],
+                            rhs=l_codes[:, g, 2 * P * b : 2 * P * (b + 1)].bitcast(E2M1),
+                            rhs_scale=l_plane[:, g, P * b : P * (b + 1)],
+                            start=(g == 0),
+                            stop=(g == 1),
+                        )
 
-        def leak(u, k):
-            half = shared[(2 * u + k // 2) % SHARED][:, Q * (k % 2) : Q * (k % 2 + 1)].bitcast(BF16)
-            nc.vector.tensor_tensor(
-                out=half.rearrange("p (c i t) -> p c t i", i=4, t=4),
-                in0=bank_of["leak", u, k][:].rearrange("p (t c i) -> p c t i", t=4, i=4),
-                in1=y[u][:, :, P * k : P * (k + 1)].rearrange("p t (c i) -> p c t i", i=4),
-                op=ADD,
-            )
+        def leak(n):
+            u, j = divmod(n, 2)
+            for k in range(2):
+                z_half = z_tiles[n % RESULTS][:, Q * k : Q * (k + 1)].bitcast(BF16)
+                bins = slice(Q * j + P * k, Q * j + P * (k + 1))
+                nc.vector.tensor_tensor(
+                    out=z_half.rearrange("p (c i t) -> p c t i", i=4, t=4),
+                    in0=bank_of["leak", n, k][:].rearrange("p (t c i) -> p c t i", t=4, i=4),
+                    in1=y[u][:, :, bins].rearrange("p t (c i) -> p c t i", i=4),
+                    op=ADD,
+                )
 
-        def quantise_z(u, k):
-            z_codes[u, k] = work.tile([P, 2 * P], U32, align_bytes=64, name="z_codes", bufs=3)
-            z_plane[u, k] = work.tile([P, 2 * P], U8, align_bytes=64, name="z_plane", bufs=3)
-            n = 2 * u + k // 2
+        def quantise_z(n):
+            z_codes[n] = work.tile([P, Q], U32, align_bytes=64, name="z_codes", bufs=3)
+            z_plane[n] = work.tile([P, Q], U8, align_bytes=64, name="z_plane", bufs=3)
             width = P if n == QUARTERS - 1 else Q
             for f0 in range(0, Q, width):
                 nc.vector.quantize_mx(
-                    out=z_codes[u, k][:, f0 : f0 + width].bitcast(E4M3),
-                    scales=z_plane[u, k][:, f0 : f0 + width],
-                    in_=shared[n % SHARED][:, 2 * f0 : 2 * (f0 + width)].bitcast(BF16),
+                    out=z_codes[n][:, f0 : f0 + width].bitcast(E4M3),
+                    scales=z_plane[n][:, f0 : f0 + width],
+                    in_=z_tiles[n % RESULTS][:, 2 * f0 : 2 * (f0 + width)].bitcast(BF16),
                 )
 
         def widen_resp():
@@ -274,191 +288,183 @@ def tile_orchestra_bleed_mix_t2_kernel(
             nc.tensor.transpose(bank[:, 0:P], resp_wide[:], ident[:])
             nc.scalar.copy(out=resp_col[:], in_=bank[:, 0 : F // P])
 
-        def mix_matmul(u, k):
-            width = turned_width(2 * u + k // 2)
-            if k % 2 * width % W == 0:
-                bank_of["mix bank"] = next_bank()
-            bank_of["mix", u, k] = bank_of["mix bank"][:, k % 2 * width % W : k % 2 * width % W + width]
-            nc.tensor.matmul_mx(
-                out=bank_of["mix", u, k],
-                lhsT=z_codes[u, k - k % 2][:, P * (k % 2) : P * (k % 2 + 1)].bitcast(E4M3),
-                lhsT_scale=z_plane[u, k - k % 2][:, P * (k % 2) : P * (k % 2 + 1)],
-                rhs=m_codes[:, 0 : 2 * width].bitcast(E2M1),
-                rhs_scale=m_plane[:, 0:width],
-                start=True,
-                stop=True,
-            )
-
-        def mix_by_microphones(u, k):
-            if turned_width(2 * u + k // 2) == C:
-                return
-            bank = next_bank()
-            bank_of["microphones", u, k] = bank
-            for dm in range(2):
+        def mix_matmuls(n):
+            width = turned_width(n)
+            for k in range(2):
+                start = k * width % W
+                if start == 0:
+                    bank = next_bank()
+                bank_of["mix", n, k] = bank[:, start : start + width]
                 nc.tensor.matmul_mx(
-                    out=bank[:, Q * dm : Q * (dm + 1)],
-                    lhsT=m_codes[:, 2 * P * (2 + dm) : 2 * P * (3 + dm)].bitcast(E2M1),
-                    lhsT_scale=m_plane[:, P * (2 + dm) : P * (3 + dm)],
-                    rhs=z_codes[u, k][:].bitcast(E4M3),
-                    rhs_scale=z_plane[u, k][:],
+                    out=bank_of["mix", n, k],
+                    lhsT=z_codes[n][:, P * k : P * (k + 1)].bitcast(E4M3),
+                    lhsT_scale=z_plane[n][:, P * k : P * (k + 1)],
+                    rhs=m_codes[:, 0 : 2 * width].bitcast(E2M1),
+                    rhs_scale=m_plane[:, 0:width],
                     start=True,
                     stop=True,
                 )
-
-        def respond_by_microphones(u, k):
-            n = 2 * u + k // 2
-            if turned_width(n) == C:
-                return
-            copied[n, 2] = work.tile([P, W], F32, name="copied", bufs=6)
-            nc.vector.tensor_tensor(
-                out=copied[n, 2][:].rearrange("p (m f) -> p m f", m=2),
-                in0=bank_of["microphones", u, k][:].rearrange("p (m f) -> p m f", m=2),
-                in1=resp_all[:, Q * (n % 4) : Q * (n % 4 + 1)].unsqueeze(1).to_broadcast([P, 2, Q]),
-                op=MULT,
-            )
-
-        def respond(u, k):
-            scaled[u, k] = work.tile([P, turned_width(2 * u + k // 2)], F32, align_bytes=64, name="scaled", bufs=4)
-            b = 4 * (u % 2) + k
-            nc.scalar.activation(
-                out=scaled[u, k][:], in_=bank_of["mix", u, k], func=COPY, scale=resp_col[:, b : b + 1]
-            )
-
-        def turn_back(n, m):
-            if P * m >= turned_width(n):
-                return
-            u, k = n // 2, 2 * (n % 2)
-            bank = next_bank()
-            bank_of["back", n, m] = bank
-            for dm in range(2):
-                for dk in range(2):
-                    nc.tensor.transpose(
-                        bank[:, Q * dm + P * dk : Q * dm + P * (dk + 1)],
-                        scaled[u, k + dk][:, P * (m + dm) : P * (m + dm + 1)],
-                        ident[:],
+            if width < C:
+                bank_of["unturned", n] = next_bank()
+                for m in range(2):
+                    nc.tensor.matmul_mx(
+                        out=bank_of["unturned", n][:, Q * m : Q * (m + 1)],
+                        lhsT=m_codes[:, 2 * P * (2 + m) : 2 * P * (3 + m)].bitcast(E2M1),
+                        lhsT_scale=m_plane[:, P * (2 + m) : P * (3 + m)],
+                        rhs=z_codes[n][:].bitcast(E4M3),
+                        rhs_scale=z_plane[n][:],
+                        start=True,
+                        stop=True,
                     )
 
-        def add_record(engine, n, m, first, result):
-            r, bins = n // 4, slice(Q * (n % 4), Q * (n % 4 + 1))
-            result = result.rearrange("p (m f) -> p m f", m=2)
-            engine.tensor_tensor(
-                out=result, in0=first.rearrange("p (m f) -> p m f", m=2), in1=recs[r][:, m : m + 2, bins], op=ADD
-            )
-            nc.sync.dma_start(out=out.rearrange("(m c) r f -> c m r f", c=P)[:, m : m + 2, r, bins], in_=result)
-            if (n, m) == (3, 2):
-                load_rec(3)
+        def respond(n):
+            for k in range(2):
+                scaled[n, k] = work.tile([P, turned_width(n)], F32, align_bytes=64, name="scaled", bufs=4)
+                b = 2 * (n % 4) + k
+                nc.scalar.activation(
+                    out=scaled[n, k][:], in_=bank_of["mix", n, k], func=COPY, scale=resp_col[:, b : b + 1]
+                )
 
-        def add_record_vector(n, m):
-            if (n, m) == (QUARTERS - 1, 2):
+        def respond_unturned(n):
+            if turned_width(n) < C:
+                unrecorded[n] = work.tile([P, W], F32, name="unrecorded", bufs=6)
+                nc.vector.tensor_tensor(
+                    out=unrecorded[n][:].rearrange("p (m f) -> p m f", m=2),
+                    in0=bank_of["unturned", n][:].rearrange("p (m f) -> p m f", m=2),
+                    in1=resp_all[:, Q * (n % 4) : Q * (n % 4 + 1)].unsqueeze(1).to_broadcast([P, 2, Q]),
+                    op=MULT,
+                )
+
+        def turn_back(n):
+            for m in range(0, turned_width(n) // P, 2):
+                bank_of["back", n, m] = next_bank()
                 for dm in range(2):
-                    result = work.tile([P, Q], F32, name="last")
-                    r, bins = n // 4, slice(Q * (n % 4), Q * (n % 4 + 1))
-                    nc.vector.tensor_tensor(
-                        out=result[:], in0=bank_of["back", n, m][:, Q * dm : Q * (dm + 1)], in1=recs[r][:, m + dm, bins], op=ADD
-                    )
-                    nc.sync.dma_start(out=out[P * (m + dm) : P * (m + dm + 1), r, bins], in_=result[:])
-            elif not on_gpsimd(n, m):
-                result = work.tile([P, W], F32, name="result", bufs=RESULTS)
-                add_record(nc.vector, n, m, bank_of["back", n, m][:], result[:])
+                    for k in range(2):
+                        nc.tensor.transpose(
+                            bank_of["back", n, m][:, Q * dm + P * k : Q * dm + P * (k + 1)],
+                            scaled[n, k][:, P * (m + dm) : P * (m + dm + 1)],
+                            ident[:],
+                        )
 
-        def copy_back(n, m):
-            if on_gpsimd(n, m) and P * m < turned_width(n):
-                copied[n, m] = work.tile([P, W], F32, name="copied", bufs=6)
-                nc.scalar.copy(out=copied[n, m][:], in_=bank_of["back", n, m][:])
+        def copy_back(n):
+            if on_gpsimd(n, 2) and turned_width(n) == C:
+                unrecorded[n] = work.tile([P, W], F32, name="unrecorded", bufs=6)
+                nc.scalar.copy(out=unrecorded[n][:], in_=bank_of["back", n, 2][:])
 
-        def add_record_gpsimd(n, m, quantised):
-            if on_gpsimd(n, m):
-                add_record(nc.gpsimd, n, m, copied[n, m][:], shared[quantised % SHARED][:] if m == 2 else copied[n, m][:])
+        def add_record(engine, n, m, groups, first, result):
+            r, bins = n // 4, slice(Q * (n % 4), Q * (n % 4 + 1))
+            result = result.rearrange("p (m f) -> p m f", m=groups)
+            engine.tensor_tensor(
+                out=result,
+                in0=first.rearrange("p (m f) -> p m f", m=groups),
+                in1=recs[r][:, m : m + groups, bins],
+                op=ADD,
+            )
+            nc.sync.dma_start(out=out.rearrange("(m c) r f -> c m r f", c=P)[:, m : m + groups, r, bins], in_=result)
+
+        def add_record_vector(n):
+            for m in (0, 2):
+                if (n, m) == (QUARTERS - 1, 2):
+                    for dm in range(2):
+                        result = work.tile([P, Q], F32, name="last_result")
+                        add_record(nc.vector, n, m + dm, 1, bank_of["back", n, m][:, Q * dm : Q * (dm + 1)], result[:])
+                elif not on_gpsimd(n, m):
+                    result = work.tile([P, W], F32, name="result", bufs=RESULTS)
+                    add_record(nc.vector, n, m, 2, bank_of["back", n, m][:], result[:])
+
+        def add_record_gpsimd(n, quantised):
+            if on_gpsimd(n, 2):
+                add_record(nc.gpsimd, n, 2, 2, unrecorded[n][:], z_tiles[quantised % RESULTS][:])
+            if n == 3:
+                load_rec(3)
 
         def at(stage, n, *rest):
             if 0 <= n < QUARTERS:
                 stage(n, *rest)
 
-        def pair(stage, n, *offsets):
-            if 0 <= n < QUARTERS:
-                for i in offsets:
-                    stage(n // 2, 2 * (n % 2) + i)
-
         reorder_a_codes()
         interleave(0, 0, Q, "vector")
-        interleave(1, 0, P, "vector")
-        interleave(1, P, Q, "scalar")
+        interleave(1, 0, Q // 2, "vector")
+        interleave(1, Q // 2, Q, "scalar")
         reorder_a_scales()
         quantise_x(0)
         quantise_x(1)
-        pair(bleed_matmul, 0, 0, 1)
-        pair(bleed_matmul, 1, 0, 1)
+        bleed_matmuls(0)
+        bleed_matmuls(1)
         interleave(2, 0, Q, "vector")
         interleave(3, 0, Q, "scalar")
         quantise_x(2)
         nc.vector.tensor_copy(out=damp_col[:], in_=damp_arrived[:])
         quantise_x(3)
-        pair(bleed_matmul, 2, 0, 1)
-        pair(bleed_matmul, 3, 0, 1)
-        for n in range(4, 7):
-            interleave(n, 0, Q, "gpsimd")
-        for n in range(4):
-            pair(bleed, n, 0, 1)
-            pair(round_y, n, 0)
-            if n < 2:
-                pair(turn_y, n, 0)
+        bleed_matmuls(2)
+        bleed_matmuls(3)
+        interleave(4, 0, Q, "gpsimd")
+        interleave(5, 0, Q, "gpsimd")
+        for n in range(3):
+            bleed(n)
+            round_y(n)
+        turn_y(0)
         quantise_x(4)
         quantise_x(5)
+        interleave(6, 0, Q, "gpsimd")
+        bleed_matmuls(4)
+        turn_y(1)
+        bleed(3)
+        gather_y(0)
+        round_y(3)
+        turn_y(2)
+        bleed_matmuls(5)
+        turn_y(3)
+        for n in range(1, 4):
+            gather_y(n)
+        widen_resp()
+        bleed(4)
         interleave(7, 0, Q, "vector")
         quantise_x(6)
+        quantise_y(0)
         quantise_x(7)
+        quantise_y(1)
+        bleed_matmuls(6)
+        round_y(4)
+        bleed(5)
+        quantise_y(2)
+        quantise_y(3)
         interleave(9, 0, Q, "gpsimd")
-        pair(bleed_matmul, 4, 0, 1)
-        pair(turn_y, 2, 0)
-        pair(turn_y, 3, 0)
-        pair(gather_y, 0, 0)
-        pair(gather_y, 1, 0)
-        widen_resp()
-        pair(gather_y, 2, 0)
-        pair(gather_y, 3, 0)
-        pair(bleed_matmul, 5, 0, 1)
-        pair(bleed, 4, 0, 1)
-        pair(quantise_y, 0, 0)
-        pair(quantise_y, 1, 0)
-        pair(round_y, 4, 0)
-        pair(bleed, 5, 0, 1)
-        pair(bleed_matmul, 6, 0, 1)
-        pair(quantise_y, 2, 0)
-        pair(quantise_y, 3, 0)
-        pair(round_y, 5, 0)
+        round_y(5)
         interleave(8, 0, Q, "scalar")
-        for n in range(6, QUARTERS + 9):
-            if n >= 7:
-                pair(bleed_matmul, n, 0, 1)
-            pair(leak_matmul, n - 6, 0, 1)
-            pair(mix_matmul, n - 7, 0, 1)
-            pair(mix_by_microphones, n - 7, 0)
-            pair(bleed, n, 0, 1)
-            if n == 6:
-                pair(turn_y, 4, 0)
+
+        for n in range(LEAK_LAG, QUARTERS + BACK_LAG):
+            first = n == LEAK_LAG
+            if not first:
+                at(bleed_matmuls, n)
+            at(leak_matmuls, n - LEAK_LAG)
+            at(mix_matmuls, n - MIX_LAG)
+            at(bleed, n)
+            if first:
+                turn_y(n - 2)
                 turn_resp()
-                pair(gather_y, 4, 0)
-            pair(round_y, n, 0)
-            pair(respond, n - 7, 0, 1)
-            pair(turn_y, n - 1, 0)
-            at(turn_back, n - 8, 0)
-            at(turn_back, n - 8, 2)
-            pair(leak, n - 6, 0, 1)
-            pair(respond_by_microphones, n - 7, 0)
-            if n == 6:
-                quantise_x(8)
-            pair(quantise_y, n - 2, 0)
-            at(quantise_x, n + 3)
-            pair(quantise_z, n - 6, 0)
-            pair(gather_y, n - 1, 0)
-            at(copy_back, n - 8, 0)
-            at(copy_back, n - 8, 2)
-            split = SPLITS.get(n, Q)
-            if split > 0:
-                at(interleave, n + 4, 0, split, "gpsimd")
-            if split < Q:
-                at(interleave, n + 4, split, Q, "scalar")
-            at(add_record_vector, n - 8, 0)
-            at(add_record_vector, n - 8, 2)
-            at(add_record_gpsimd, n - 9, 2, n - 6)
-            at(add_record_gpsimd, n - 9, 0, n - 6)
+                gather_y(n - 2)
+            at(round_y, n)
+            at(respond, n - MIX_LAG)
+            at(turn_y, n - 1)
+            at(turn_back, n - BACK_LAG)
+            at(leak, n - LEAK_LAG)
+            at(respond_unturned, n - MIX_LAG)
+            if first:
+                quantise_x(n + X_LEAD - 1)
+                quantise_z(0)
+                quantise_x(n + X_LEAD)
+                quantise_y(n - 2)
+            else:
+                at(quantise_y, n - 2)
+                at(quantise_x, n + X_LEAD)
+                at(quantise_z, n - LEAK_LAG)
+            at(gather_y, n - 1)
+            at(copy_back, n - BACK_LAG)
+            if n > BACK_LAG:
+                at(interleave, n + X_LEAD + 1, 0, GPSIMD_BINS, "gpsimd")
+                at(interleave, n + X_LEAD + 1, GPSIMD_BINS, Q, "scalar")
+            else:
+                interleave(n + X_LEAD + 1, 0, Q, "gpsimd")
+            at(add_record_vector, n - BACK_LAG)
+            at(add_record_gpsimd, n - BACK_LAG - 1, n - LEAK_LAG)

@@ -360,7 +360,8 @@ def tile_orchestra_bleed_mix_t2_kernel(
                 in1=recs[r][:, m : m + groups, bins],
                 op=ADD,
             )
-            nc.sync.dma_start(out=out.rearrange("(m c) r f -> c m r f", c=P)[:, m : m + groups, r, bins], in_=result)
+            queue = nc.scalar if n == QUARTERS - 1 and m != 2 else nc.sync
+            queue.dma_start(out=out.rearrange("(m c) r f -> c m r f", c=P)[:, m : m + groups, r, bins], in_=result)
 
         def add_record_vector(n):
             for m in (0, 2):

@@ -24,16 +24,22 @@ QUARTERS = 4 * T
 FLOPS = 2 * (2 * S * S * T * F + S * T * F * F)
 
 BANKS = 8
-RESULTS = 8
+SHEETS = 64
+RESTING = 6
 
 LEAK_LAG = 6
 MIX_LAG = LEAK_LAG + 1
 BACK_LAG = LEAK_LAG + 2
 X_LEAD = 3
 
-GPSIMD_QUARTERS = 12
-FIRST_HALF_TURNED = 7
-GPSIMD_BINS = 192
+TURNED_VECTOR, TURNED_GPSIMD, UNTURNED_GPSIMD, UNTURNED_VECTOR = "a", "g", "b", "c"
+WAYS = "ag ag ag ag ag ag ag ab ag ab ag ab aa aa aa aa".split()
+GA = {}
+GB = {9:192,10:192,11:192}
+
+
+def way(n):
+    return WAYS[n]
 
 
 def tile_orchestra_bleed_mix_t2_kernel(
@@ -61,26 +67,16 @@ def tile_orchestra_bleed_mix_t2_kernel(
         resp_all = keep.tile([P, F], BF16, align_bytes=64, name="resp_all")
         resp_col = keep.tile([P, F // P], F32, name="resp_col")
         ident = keep.tile([P, P], F32, align_bytes=64, name="ident")
-        z_tiles = []
-        for i in range(RESULTS):
-            z_tile = keep.tile([P, W], F32, align_bytes=64, name="z%d" % i)
-            z_tiles.append(z_tile)
-        staged = []
-        for i in range(5):
-            staged_tile = keep.tile([P, 4 * Q], BF16, align_bytes=64, name="staged%d" % i)
-            staged.append(staged_tile)
 
-        def grouped(n):
-            if n < 4:
-                return staged[n]
-            return staged[{4: 3, 5: 0, 6: 0, 7: 1, 8: 2}.get(n, 4)]
+        idle_sheets, spare_sheets = [], []
+        for i in range(SHEETS):
+            sheet = keep.tile([P, W], F32, align_bytes=64, name="sheet%d" % i)
+            spare_sheets.append(sheet)
 
-        def turned_width(n):
-            half = FIRST_HALF_TURNED <= n < GPSIMD_QUARTERS and (n - FIRST_HALF_TURNED) % 2 == 0
-            return C // 2 if half else C
-
-        def on_gpsimd(n, m):
-            return m == 2 and n < GPSIMD_QUARTERS
+        def take_sheet(behind_quantising=False):
+            if behind_quantising:
+                return idle_sheets.pop()
+            return idle_sheets.pop(0) if len(idle_sheets) > RESTING else spare_sheets.pop(0)
 
         def as_int32(ap):
             return ap.bitcast(I32)
@@ -92,26 +88,38 @@ def tile_orchestra_bleed_mix_t2_kernel(
         nc.vector.memset(resp_rows[:], 0.0)
         make_identity(nc, ident[:], nomemset=True)
 
-        raw, recs = {}, {}
+        raw, loaded = {}, {}
 
         def load_x(u, halves, queue=nc.sync):
-            loaded = keep.tile([P, 4, halves * W], BF16, align_bytes=64, name="raw%d" % u)
+            loaded[u] = keep.tile([P, 4, halves * W], BF16, align_bytes=64, name="raw%d" % u)
             bins = slice(W * (u % 2), W * (u % 2 + halves))
-            queue.dma_start(out=loaded[:], in_=x.rearrange("(p t) r f -> p t r f", t=4)[:, :, u // 2, bins])
+            queue.dma_start(out=loaded[u][:], in_=x.rearrange("(p t) r f -> p t r f", t=4)[:, :, u // 2, bins])
             for g in range(halves):
-                raw[u + g] = loaded[:, :, W * g : W * (g + 1)]
+                raw[u + g] = loaded[u][:, :, W * g : W * (g + 1)]
 
-        def load_rec(r):
-            recs[r] = work.tile([P, C // P, F], BF16, align_bytes=64, name="rec", bufs=3)
-            nc.sync.dma_start(out=recs[r][:], in_=rec.rearrange("(m c) r f -> c m r f", c=P)[:, :, r, :])
+        def load_rec(n):
+            for u in loaded:
+                width = loaded[u].shape[2]
+                if n == 2 * u + width // Q - 1:
+                    bins = slice(W * (u % 2), W * (u % 2) + width)
+                    nc.sync.dma_start(
+                        out=loaded[u][:], in_=rec.rearrange("(m c) r f -> c m r f", c=P)[:, :, u // 2, bins]
+                    )
 
-        load_x(0, 1, nc.scalar)
+        def load_scales(plane, scales):
+            for q in range(4):
+                rows = slice(32 * q, 32 * q + 4)
+                if scales.shape[0] == 1:
+                    nc.sync.dma_start(out=as_int32(plane[rows, :]), in_=as_int32(scales[0, 4 * q : 4 * q + 4, :]))
+                else:
+                    nc.sync.dma_start(
+                        out=as_int32(plane[rows, :, :]),
+                        in_=as_int32(scales[:, 4 * q : 4 * q + 4, :].rearrange("g q n -> q g n")),
+                    )
+
         nc.sync.dma_start(out=as_int32(a_arrived[:]), in_=as_int32(a_words[0]))
-        for q in range(4):
-            nc.sync.dma_start(
-                out=as_int32(a_scales_arrived[32 * q : 32 * q + 4, :]),
-                in_=as_int32(a_scales[0, 4 * q : 4 * q + 4, :]),
-            )
+        load_x(0, 1)
+        load_scales(a_scales_arrived, a_scales)
         load_x(1, 1)
         nc.sync.dma_start(out=damp_arrived[:], in_=damp.rearrange("(p t) -> p t", t=4))
         load_x(2, 1)
@@ -119,23 +127,14 @@ def tile_orchestra_bleed_mix_t2_kernel(
         load_x(4, 2)
         nc.sync.dma_start(out=resp_rows[0 : F // P, :], in_=resp.rearrange("(b q) -> b q", q=P))
         nc.sync.dma_start(out=as_int32(l_codes[:]), in_=as_int32(l_words.rearrange("g p n -> p g n")))
-        for q in range(4):
-            nc.sync.dma_start(
-                out=as_int32(l_plane[32 * q : 32 * q + 4, :, :]),
-                in_=as_int32(l_scales[:, 4 * q : 4 * q + 4, :].rearrange("g q n -> q g n")),
-            )
+        load_scales(l_plane, l_scales)
         nc.sync.dma_start(out=as_int32(m_codes[:]), in_=as_int32(m_words[0]))
-        for q in range(4):
-            nc.sync.dma_start(
-                out=as_int32(m_plane[32 * q : 32 * q + 4, :]), in_=as_int32(m_scales[0, 4 * q : 4 * q + 4, :])
-            )
+        load_scales(m_plane, m_scales)
         load_x(6, 2)
-        for r in range(3):
-            load_rec(r)
         nc.sync.dma_start(out=resp_all[:], in_=resp.partition_broadcast(P))
 
-        def reorder_a_codes():
-            nc.vector.tensor_copy(
+        def reorder_a_codes(copy):
+            copy(
                 out=a_codes[:].bitcast(U16).rearrange("p (t m) -> p t m", t=4),
                 in_=a_arrived[:].bitcast(U16).rearrange("p (m t) -> p t m", t=4),
             )
@@ -146,14 +145,21 @@ def tile_orchestra_bleed_mix_t2_kernel(
                 in_=a_scales_arrived[:].rearrange("p (m t) -> p t m", t=4),
             )
 
-        x_codes, x_plane, y, y_bf16, y_turned, y_codes, y_plane = {}, {}, {}, {}, {}, {}, {}
-        z_codes, z_plane, scaled, unrecorded, bank_of = {}, {}, {}, {}, {}
+        grouped, x_codes, x_plane, y, y_bf16, y_turned, y_codes, y_plane = {}, {}, {}, {}, {}, {}, {}, {}
+        unstored, waiting = [], []
+        z, z_codes, z_plane, scaled, unrecorded, bank_of = {}, {}, {}, {}, {}, {}
+
+        turns = []
 
         def next_bank():
-            return psum.tile([P, W], F32, name="bank", bufs=BANKS)
+            i = turns.pop(0)
+            turns.append(i)
+            return psum.tile([P, W], F32, name="bank%d" % i)
 
-        def interleave(n, f0, f1, engine):
-            out_ap = grouped(n)[:, 4 * f0 : 4 * f1].rearrange("p (f t) -> p f t", t=4)
+        def interleave(n, engine, behind_quantising=False, f0=0, f1=Q):
+            if n not in grouped:
+                grouped[n] = take_sheet(behind_quantising)
+            out_ap = grouped[n][:].bitcast(BF16)[:, 4 * f0 : 4 * f1].rearrange("p (f t) -> p f t", t=4)
             in_ap = raw[n // 2][:, :, Q * (n % 2) + f0 : Q * (n % 2) + f1]
             if engine == "gpsimd":
                 nc.gpsimd.tensor_scalar(
@@ -174,8 +180,9 @@ def tile_orchestra_bleed_mix_t2_kernel(
             nc.vector.quantize_mx(
                 out=x_codes[u][:, Q * j : Q * (j + 1)].bitcast(E4M3),
                 scales=x_plane[u][:, Q * j : Q * (j + 1)],
-                in_=grouped(n)[:],
+                in_=grouped[n][:].bitcast(BF16),
             )
+            idle_sheets.append(grouped[n])
 
         def bleed_matmuls(n):
             u, j = divmod(n, 2)
@@ -191,11 +198,11 @@ def tile_orchestra_bleed_mix_t2_kernel(
                     stop=True,
                 )
 
-        def bleed(n):
+        def bleed(n, t0=0, t1=2):
             u, j = divmod(n, 2)
-            if j == 0:
+            if u not in y:
                 y[u] = work.tile([P, 4, W], F32, align_bytes=64, name="y", bufs=5)
-            for t in (2 * j, 2 * j + 1):
+            for t in range(2 * j + t0, 2 * j + t1):
                 nc.vector.scalar_tensor_tensor(
                     out=y[u][:, t, :],
                     in0=bank_of["bleed", u, t][:],
@@ -205,27 +212,27 @@ def tile_orchestra_bleed_mix_t2_kernel(
                     op1=ADD,
                 )
 
-        def round_y(n):
+        def round_y(n, t0=0, t1=2):
             u, j = divmod(n, 2)
-            y_bf16[n] = work.tile([P, 2 * W], BF16, align_bytes=64, name="y_bf16", bufs=4)
+            if n not in y_bf16:
+                y_bf16[n] = take_sheet()
             nc.scalar.copy(
-                out=y_bf16[n][:].rearrange("p (t h w e) -> p t h w e", t=2, h=2, e=2),
-                in_=y[u][:, 2 * j : 2 * j + 2, :].rearrange("p t (w h e) -> p t h w e", h=2, e=2),
+                out=y_bf16[n][:].bitcast(BF16)[:, W * t0 : W * t1].rearrange("p (t h w e) -> p t h w e", w=P, h=2, e=2),
+                in_=y[u][:, 2 * j + t0 : 2 * j + t1, :].rearrange("p t (w h e) -> p t h w e", h=2, e=2),
             )
 
         def turn_y(n):
             bank_of["turn", n] = next_bank()
             for i in range(4):
-                pairs = y_bf16[n][:, 2 * P * i : 2 * P * (i + 1)].bitcast(F32)
-                nc.tensor.transpose(bank_of["turn", n][:, P * i : P * (i + 1)], pairs, ident[:])
+                nc.tensor.transpose(
+                    bank_of["turn", n][:, P * i : P * (i + 1)], y_bf16[n][:, P * i : P * (i + 1)], ident[:]
+                )
+            idle_sheets.append(y_bf16[n])
 
         def gather_y(n):
-            if n == 3:
-                y_turned[n] = staged[4]
-            else:
-                y_turned[n] = work.tile([P, 2 * S], BF16, align_bytes=64, name="y_turned", bufs=4)
+            y_turned[n] = take_sheet()
             nc.scalar.copy(
-                out=y_turned[n][:].bitcast(F32).rearrange("w (t p h) -> w t p h", t=2, h=2),
+                out=y_turned[n][:].rearrange("w (t p h) -> w t p h", t=2, h=2),
                 in_=bank_of["turn", n][:].rearrange("w (t h p) -> w t p h", t=2, h=2),
             )
 
@@ -237,8 +244,9 @@ def tile_orchestra_bleed_mix_t2_kernel(
             nc.vector.quantize_mx(
                 out=y_codes[u][:, Q * j : Q * (j + 1)].bitcast(E4M3),
                 scales=y_plane[u][:, Q * j : Q * (j + 1)],
-                in_=y_turned[n][:],
+                in_=y_turned[n][:].bitcast(BF16),
             )
+            idle_sheets.append(y_turned[n])
 
         def leak_matmuls(n):
             r = n // 4
@@ -259,8 +267,9 @@ def tile_orchestra_bleed_mix_t2_kernel(
 
         def leak(n):
             u, j = divmod(n, 2)
+            z[n] = take_sheet()
             for k in range(2):
-                z_half = z_tiles[n % RESULTS][:, Q * k : Q * (k + 1)].bitcast(BF16)
+                z_half = z[n][:, Q * k : Q * (k + 1)].bitcast(BF16)
                 bins = slice(Q * j + P * k, Q * j + P * (k + 1))
                 nc.vector.tensor_tensor(
                     out=z_half.rearrange("p (c i t) -> p c t i", i=4, t=4),
@@ -277,8 +286,9 @@ def tile_orchestra_bleed_mix_t2_kernel(
                 nc.vector.quantize_mx(
                     out=z_codes[n][:, f0 : f0 + width].bitcast(E4M3),
                     scales=z_plane[n][:, f0 : f0 + width],
-                    in_=z_tiles[n % RESULTS][:, 2 * f0 : 2 * (f0 + width)].bitcast(BF16),
+                    in_=z[n][:, 2 * f0 : 2 * (f0 + width)].bitcast(BF16),
                 )
+            idle_sheets.append(z[n])
 
         def widen_resp():
             nc.scalar.copy(out=resp_wide[:], in_=resp_rows[:])
@@ -288,9 +298,16 @@ def tile_orchestra_bleed_mix_t2_kernel(
             nc.tensor.transpose(bank[:, 0:P], resp_wide[:], ident[:])
             nc.scalar.copy(out=resp_col[:], in_=bank[:, 0 : F // P])
 
+        def turned(n):
+            return [h for h in range(2) if way(n)[h] in (TURNED_VECTOR, TURNED_GPSIMD)]
+
+        def unturned(n):
+            return [h for h in range(2) if h not in turned(n)]
+
         def mix_matmuls(n):
-            width = turned_width(n)
-            for k in range(2):
+            width = Q * len(turned(n))
+            for k in range(2 if width else 0):
+                c0 = Q * turned(n)[0]
                 start = k * width % W
                 if start == 0:
                     bank = next_bank()
@@ -299,18 +316,19 @@ def tile_orchestra_bleed_mix_t2_kernel(
                     out=bank_of["mix", n, k],
                     lhsT=z_codes[n][:, P * k : P * (k + 1)].bitcast(E4M3),
                     lhsT_scale=z_plane[n][:, P * k : P * (k + 1)],
-                    rhs=m_codes[:, 0 : 2 * width].bitcast(E2M1),
-                    rhs_scale=m_plane[:, 0:width],
+                    rhs=m_codes[:, 2 * c0 : 2 * (c0 + width)].bitcast(E2M1),
+                    rhs_scale=m_plane[:, c0 : c0 + width],
                     start=True,
                     stop=True,
                 )
-            if width < C:
-                bank_of["unturned", n] = next_bank()
-                for m in range(2):
+            for h in unturned(n):
+                bank_of["unturned", n, h] = next_bank()
+                for dm in range(2):
+                    m = 2 * h + dm
                     nc.tensor.matmul_mx(
-                        out=bank_of["unturned", n][:, Q * m : Q * (m + 1)],
-                        lhsT=m_codes[:, 2 * P * (2 + m) : 2 * P * (3 + m)].bitcast(E2M1),
-                        lhsT_scale=m_plane[:, P * (2 + m) : P * (3 + m)],
+                        out=bank_of["unturned", n, h][:, Q * dm : Q * (dm + 1)],
+                        lhsT=m_codes[:, 2 * P * m : 2 * P * (m + 1)].bitcast(E2M1),
+                        lhsT_scale=m_plane[:, P * m : P * (m + 1)],
                         rhs=z_codes[n][:].bitcast(E4M3),
                         rhs_scale=z_plane[n][:],
                         start=True,
@@ -318,38 +336,45 @@ def tile_orchestra_bleed_mix_t2_kernel(
                     )
 
         def respond(n):
-            for k in range(2):
-                scaled[n, k] = work.tile([P, turned_width(n)], F32, align_bytes=64, name="scaled", bufs=4)
+            width = Q * len(turned(n))
+            for k in range(2 if width else 0):
+                start = k * width % W
+                if start == 0:
+                    sheet = take_sheet()
+                    scaled.setdefault(n, []).append(sheet)
+                scaled[n, k] = sheet[:, start : start + width]
                 b = 2 * (n % 4) + k
                 nc.scalar.activation(
-                    out=scaled[n, k][:], in_=bank_of["mix", n, k], func=COPY, scale=resp_col[:, b : b + 1]
+                    out=scaled[n, k], in_=bank_of["mix", n, k], func=COPY, scale=resp_col[:, b : b + 1]
                 )
 
         def respond_unturned(n):
-            if turned_width(n) < C:
-                unrecorded[n] = work.tile([P, W], F32, name="unrecorded", bufs=6)
+            for h in unturned(n):
+                unrecorded[n, h] = take_sheet()
                 nc.vector.tensor_tensor(
-                    out=unrecorded[n][:].rearrange("p (m f) -> p m f", m=2),
-                    in0=bank_of["unturned", n][:].rearrange("p (m f) -> p m f", m=2),
+                    out=unrecorded[n, h][:].rearrange("p (m f) -> p m f", m=2),
+                    in0=bank_of["unturned", n, h][:].rearrange("p (m f) -> p m f", m=2),
                     in1=resp_all[:, Q * (n % 4) : Q * (n % 4 + 1)].unsqueeze(1).to_broadcast([P, 2, Q]),
                     op=MULT,
                 )
 
         def turn_back(n):
-            for m in range(0, turned_width(n) // P, 2):
-                bank_of["back", n, m] = next_bank()
+            for i, h in enumerate(turned(n)):
+                bank_of["back", n, h] = next_bank()
                 for dm in range(2):
                     for k in range(2):
                         nc.tensor.transpose(
-                            bank_of["back", n, m][:, Q * dm + P * k : Q * dm + P * (k + 1)],
-                            scaled[n, k][:, P * (m + dm) : P * (m + dm + 1)],
+                            bank_of["back", n, h][:, Q * dm + P * k : Q * dm + P * (k + 1)],
+                            scaled[n, k][:, P * (2 * i + dm) : P * (2 * i + dm + 1)],
                             ident[:],
                         )
+            idle_sheets.extend(scaled.get(n, []))
 
         def copy_back(n):
-            if on_gpsimd(n, 2) and turned_width(n) == C:
-                unrecorded[n] = work.tile([P, W], F32, name="unrecorded", bufs=6)
-                nc.scalar.copy(out=unrecorded[n][:], in_=bank_of["back", n, 2][:])
+            for h in range(2):
+                if way(n)[h] == TURNED_GPSIMD:
+                    unrecorded[n, h] = take_sheet()
+                    nc.scalar.copy(out=unrecorded[n, h][:], in_=bank_of["back", n, h][:])
 
         def add_record(engine, n, m, groups, first, result):
             r, bins = n // 4, slice(Q * (n % 4), Q * (n % 4 + 1))
@@ -357,97 +382,127 @@ def tile_orchestra_bleed_mix_t2_kernel(
             engine.tensor_tensor(
                 out=result,
                 in0=first.rearrange("p (m f) -> p m f", m=groups),
-                in1=recs[r][:, m : m + groups, bins],
+                in1=raw[n // 2][:, m : m + groups, Q * (n % 2) : Q * (n % 2 + 1)],
                 op=ADD,
             )
-            queue = nc.scalar if n == QUARTERS - 1 and m != 2 else nc.sync
-            queue.dma_start(out=out.rearrange("(m c) r f -> c m r f", c=P)[:, m : m + groups, r, bins], in_=result)
+            return out.rearrange("(m c) r f -> c m r f", c=P)[:, m : m + groups, r, bins], result
 
         def add_record_vector(n):
-            for m in (0, 2):
-                if (n, m) == (QUARTERS - 1, 2):
-                    for dm in range(2):
-                        result = work.tile([P, Q], F32, name="last_result")
-                        add_record(nc.vector, n, m + dm, 1, bank_of["back", n, m][:, Q * dm : Q * (dm + 1)], result[:])
-                elif not on_gpsimd(n, m):
-                    result = work.tile([P, W], F32, name="result", bufs=RESULTS)
-                    add_record(nc.vector, n, m, 2, bank_of["back", n, m][:], result[:])
+            for h in range(2):
+                if way(n)[h] in (TURNED_VECTOR, UNTURNED_VECTOR):
+                    first = bank_of["back", n, h] if h in turned(n) else unrecorded[n, h]
+                    parts = 2 if (n, h) == (QUARTERS - 1, 1) else 1
+                    for dm in range(parts):
+                        result = take_sheet()
+                        cols = slice(W // parts * dm, W // parts * (dm + 1))
+                        m = 2 * h + dm
+                        target, block = add_record(nc.vector, n, m, 2 // parts, first[:, cols], result[:, 0 : W // parts])
+                        queue = nc.scalar if n == QUARTERS - 1 and m != 2 else nc.sync
+                        queue.dma_start(out=target, in_=block)
+                        spare_sheets.append(result)
+                    if h in unturned(n):
+                        idle_sheets.append(unrecorded[n, h])
 
-        def add_record_gpsimd(n, quantised):
-            if on_gpsimd(n, 2):
-                add_record(nc.gpsimd, n, 2, 2, unrecorded[n][:], z_tiles[quantised % RESULTS][:])
-            if n == 3:
-                load_rec(3)
+        def add_record_gpsimd(groups, behind_quantising):
+            n, m = waiting[0]
+            waiting[:groups] = []
+            result = take_sheet(behind_quantising)
+            first = unrecorded[n, m // 2][:, Q * (m % 2) : Q * (m % 2 + groups)]
+            unstored.append((result, add_record(nc.gpsimd, n, m, groups, first, result[:, 0 : Q * groups])))
+            if (m + groups) % 2 == 0:
+                spare_sheets.append(unrecorded[n, m // 2])
+
+        def store_gpsimd():
+            for result, (target, block) in unstored:
+                nc.sync.dma_start(out=target, in_=block)
+                spare_sheets.append(result)
+            unstored.clear()
 
         def at(stage, n, *rest):
             if 0 <= n < QUARTERS:
                 stage(n, *rest)
 
-        reorder_a_codes()
-        interleave(0, 0, Q, "vector")
-        interleave(1, 0, Q // 2, "vector")
-        interleave(1, Q // 2, Q, "scalar")
+        bleed_banks, turn_banks = [0, 1, 2, 3], [4, 5, 6, 7]
+
+        def early(stage, banks, n):
+            turns[:] = banks
+            stage(n)
+            banks[:] = turns
+
+        reorder_a_codes(nc.vector.tensor_copy)
+        interleave(0, "vector")
+        interleave(1, "vector", False, 0, Q // 2)
+        interleave(1, "scalar", False, Q // 2, Q)
         reorder_a_scales()
         quantise_x(0)
         quantise_x(1)
-        bleed_matmuls(0)
-        bleed_matmuls(1)
-        interleave(2, 0, Q, "vector")
-        interleave(3, 0, Q, "scalar")
+        early(bleed_matmuls, bleed_banks, 0)
+        early(bleed_matmuls, bleed_banks, 1)
+        interleave(2, "vector")
+        interleave(3, "scalar")
         quantise_x(2)
         nc.vector.tensor_copy(out=damp_col[:], in_=damp_arrived[:])
         quantise_x(3)
-        bleed_matmuls(2)
-        bleed_matmuls(3)
-        interleave(4, 0, Q, "gpsimd")
-        interleave(5, 0, Q, "gpsimd")
-        for n in range(3):
-            bleed(n)
-            round_y(n)
-        turn_y(0)
+        interleave(4, "scalar")
+        interleave(5, "gpsimd", True)
+        bleed(0)
+        early(bleed_matmuls, bleed_banks, 2)
+        round_y(0)
+        bleed(1)
+        early(bleed_matmuls, bleed_banks, 3)
+        round_y(1)
+        early(turn_y, turn_banks, 0)
         quantise_x(4)
         quantise_x(5)
-        interleave(6, 0, Q, "gpsimd")
-        bleed_matmuls(4)
-        turn_y(1)
-        bleed(3)
+        interleave(6, "gpsimd", True)
+        bleed(2)
+        early(bleed_matmuls, bleed_banks, 4)
+        early(turn_y, turn_banks, 1)
         gather_y(0)
+        round_y(2)
+        bleed(3)
+        early(turn_y, turn_banks, 2)
+        early(bleed_matmuls, bleed_banks, 5)
         round_y(3)
-        turn_y(2)
-        bleed_matmuls(5)
-        turn_y(3)
+        early(turn_y, turn_banks, 3)
         for n in range(1, 4):
             gather_y(n)
-        widen_resp()
-        bleed(4)
-        interleave(7, 0, Q, "vector")
-        quantise_x(6)
         quantise_y(0)
-        quantise_x(7)
-        quantise_y(1)
-        bleed_matmuls(6)
-        round_y(4)
+        quantise_x(6)
+        interleave(7, "gpsimd", True)
+        bleed(4)
         bleed(5)
-        quantise_y(2)
-        quantise_y(3)
-        interleave(9, 0, Q, "gpsimd")
+        quantise_x(7)
+        turns[:] = bleed_banks + turn_banks
+        bleed_matmuls(6)
+        for n in range(1, 4):
+            quantise_y(n)
+        interleave(8, "gpsimd", True)
+        interleave(9, "scalar")
+        widen_resp()
+        round_y(4)
         round_y(5)
-        interleave(8, 0, Q, "scalar")
+        for n in range(LEAK_LAG):
+            load_rec(n)
 
-        for n in range(LEAK_LAG, QUARTERS + BACK_LAG):
+        for n in range(LEAK_LAG, QUARTERS + BACK_LAG + 1):
             first = n == LEAK_LAG
             if not first:
                 at(bleed_matmuls, n)
             at(leak_matmuls, n - LEAK_LAG)
             at(mix_matmuls, n - MIX_LAG)
             at(bleed, n)
+            at(load_rec, n)
             if first:
                 turn_y(n - 2)
                 turn_resp()
                 gather_y(n - 2)
             at(round_y, n)
             at(respond, n - MIX_LAG)
-            at(turn_y, n - 1)
+            if n == LEAK_LAG + 1:
+                turn_y(n - 2)
+            if not first:
+                at(turn_y, n - 1)
             at(turn_back, n - BACK_LAG)
             at(leak, n - LEAK_LAG)
             at(respond_unturned, n - MIX_LAG)
@@ -455,17 +510,32 @@ def tile_orchestra_bleed_mix_t2_kernel(
                 quantise_x(n + X_LEAD - 1)
                 quantise_z(0)
                 quantise_x(n + X_LEAD)
-                quantise_y(n - 2)
             else:
-                at(quantise_y, n - 2)
+                if n in (LEAK_LAG + 1, LEAK_LAG + 2):
+                    quantise_y(n - 3)
+                if n != LEAK_LAG + 1:
+                    at(quantise_y, n - 2)
                 at(quantise_x, n + X_LEAD)
                 at(quantise_z, n - LEAK_LAG)
-            at(gather_y, n - 1)
+            for m, kind in ((n - BACK_LAG - 1, TURNED_GPSIMD), (n - MIX_LAG, UNTURNED_GPSIMD)):
+                if 0 <= m < QUARTERS:
+                    waiting.extend((m, 2 * h + dm) for h in range(2) for dm in range(2) if way(m)[h] == kind)
+            tie = True
+            if n + X_LEAD + 1 < QUARTERS:
+                interleave(n + X_LEAD + 1, "gpsimd", True, 0, GB.get(n, Q))
+                tie = False
+            left = GA.get(n, 2)
+            while left and waiting:
+                groups = min(left, 2 - waiting[0][1] % 2)
+                add_record_gpsimd(groups, tie)
+                tie = False
+                left -= groups
+            if n == LEAK_LAG + 1:
+                gather_y(n - 2)
+            if not first:
+                at(gather_y, n - 1)
             at(copy_back, n - BACK_LAG)
-            if n > BACK_LAG:
-                at(interleave, n + X_LEAD + 1, 0, GPSIMD_BINS, "gpsimd")
-                at(interleave, n + X_LEAD + 1, GPSIMD_BINS, Q, "scalar")
-            else:
-                interleave(n + X_LEAD + 1, 0, Q, "gpsimd")
+            if n in GB:
+                interleave(n + X_LEAD + 1, "scalar", False, GB[n], Q)
             at(add_record_vector, n - BACK_LAG)
-            at(add_record_gpsimd, n - BACK_LAG - 1, n - LEAK_LAG)
+            store_gpsimd()

@@ -33,7 +33,7 @@ BACK_LAG = LEAK_LAG + 2
 X_LEAD = 3
 
 TURNED_VECTOR, TURNED_GPSIMD, UNTURNED_GPSIMD, UNTURNED_VECTOR = "a", "g", "b", "c"
-WAYS = "ag ag ag ag ag ag ag ab ag ab ag ab aa aa aa aa".split()
+WAYS = "ag ag ag ag ag ag ag ag ag ag ag ag ag aa aa aa".split()
 GA = {}
 GB = {9:192,10:192,11:192}
 
@@ -64,7 +64,6 @@ def tile_orchestra_bleed_mix_t2_kernel(
         damp_col = keep.tile([P, 4], F32, name="damp_col")
         resp_rows = keep.tile([P, P], BF16, align_bytes=64, name="resp_rows")
         resp_wide = keep.tile([P, P], F32, align_bytes=64, name="resp_wide")
-        resp_all = keep.tile([P, F], BF16, align_bytes=64, name="resp_all")
         resp_col = keep.tile([P, F // P], F32, name="resp_col")
         ident = keep.tile([P, P], F32, align_bytes=64, name="ident")
 
@@ -88,29 +87,29 @@ def tile_orchestra_bleed_mix_t2_kernel(
         nc.vector.memset(resp_rows[:], 0.0)
         make_identity(nc, ident[:], nomemset=True)
 
-        raw, loaded = {}, {}
+        frames, raw, recs = {}, {}, {}
 
-        def load_x(u, halves, queue=nc.sync):
-            loaded[u] = keep.tile([P, 4, halves * W], BF16, align_bytes=64, name="raw%d" % u)
-            bins = slice(W * (u % 2), W * (u % 2 + halves))
-            queue.dma_start(out=loaded[u][:], in_=x.rearrange("(p t) r f -> p t r f", t=4)[:, :, u // 2, bins])
-            for g in range(halves):
-                raw[u + g] = loaded[u][:, :, W * g : W * (g + 1)]
+        def load_x(u, halves):
+            r, g = divmod(u, 2)
+            if g == 0:
+                frames[r] = keep.tile([P, 4 * F], BF16, align_bytes=64, name="frame%d" % r)
+            loaded = frames[r][:, 4 * W * g : 4 * W * (g + halves)].rearrange("p (t f) -> p t f", t=4)
+            bins = slice(W * g, W * (g + halves))
+            nc.sync.dma_start(out=loaded, in_=x.rearrange("(p t) r f -> p t r f", t=4)[:, :, r, bins])
+            for i in range(halves):
+                raw[u + i] = loaded[:, :, W * i : W * (i + 1)]
 
         def load_rec(n):
-            for u in loaded:
-                width = loaded[u].shape[2]
-                if n == 2 * u + width // Q - 1:
-                    bins = slice(W * (u % 2), W * (u % 2) + width)
-                    nc.sync.dma_start(
-                        out=loaded[u][:], in_=rec.rearrange("(m c) r f -> c m r f", c=P)[:, :, u // 2, bins]
-                    )
+            r = n // 4
+            if n % 4 == 3:
+                recs[r] = frames[r][:].rearrange("p (m f) -> p m f", m=C // P)
+                nc.sync.dma_start(out=recs[r], in_=rec.rearrange("(m c) r f -> c m r f", c=P)[:, :, r, :])
 
-        def load_scales(plane, scales):
+        def load_scales(plane, scales, queue=nc.sync):
             for q in range(4):
                 rows = slice(32 * q, 32 * q + 4)
                 if scales.shape[0] == 1:
-                    nc.sync.dma_start(out=as_int32(plane[rows, :]), in_=as_int32(scales[0, 4 * q : 4 * q + 4, :]))
+                    queue.dma_start(out=as_int32(plane[rows, :]), in_=as_int32(scales[0, 4 * q : 4 * q + 4, :]))
                 else:
                     nc.sync.dma_start(
                         out=as_int32(plane[rows, :, :]),
@@ -124,14 +123,13 @@ def tile_orchestra_bleed_mix_t2_kernel(
         nc.sync.dma_start(out=damp_arrived[:], in_=damp.rearrange("(p t) -> p t", t=4))
         load_x(2, 1)
         load_x(3, 1)
-        load_x(4, 2)
         nc.sync.dma_start(out=resp_rows[0 : F // P, :], in_=resp.rearrange("(b q) -> b q", q=P))
+        load_x(4, 2)
         nc.sync.dma_start(out=as_int32(l_codes[:]), in_=as_int32(l_words.rearrange("g p n -> p g n")))
         load_scales(l_plane, l_scales)
         nc.sync.dma_start(out=as_int32(m_codes[:]), in_=as_int32(m_words[0]))
         load_scales(m_plane, m_scales)
         load_x(6, 2)
-        nc.sync.dma_start(out=resp_all[:], in_=resp.partition_broadcast(P))
 
         def reorder_a_codes(copy):
             copy(
@@ -184,9 +182,9 @@ def tile_orchestra_bleed_mix_t2_kernel(
             )
             idle_sheets.append(grouped[n])
 
-        def bleed_matmuls(n):
+        def bleed_matmuls(n, t0=0, t1=2):
             u, j = divmod(n, 2)
-            for t in (2 * j, 2 * j + 1):
+            for t in range(2 * j + t0, 2 * j + t1):
                 bank_of["bleed", u, t] = next_bank()
                 nc.tensor.matmul_mx(
                     out=bank_of["bleed", u, t][:],
@@ -296,7 +294,10 @@ def tile_orchestra_bleed_mix_t2_kernel(
         def turn_resp():
             bank = next_bank()
             nc.tensor.transpose(bank[:, 0:P], resp_wide[:], ident[:])
-            nc.scalar.copy(out=resp_col[:], in_=bank[:, 0 : F // P])
+            bank_of["resp"] = bank
+
+        def keep_resp():
+            nc.scalar.copy(out=resp_col[:], in_=bank_of["resp"][:, 0 : F // P])
 
         def turned(n):
             return [h for h in range(2) if way(n)[h] in (TURNED_VECTOR, TURNED_GPSIMD)]
@@ -321,19 +322,6 @@ def tile_orchestra_bleed_mix_t2_kernel(
                     start=True,
                     stop=True,
                 )
-            for h in unturned(n):
-                bank_of["unturned", n, h] = next_bank()
-                for dm in range(2):
-                    m = 2 * h + dm
-                    nc.tensor.matmul_mx(
-                        out=bank_of["unturned", n, h][:, Q * dm : Q * (dm + 1)],
-                        lhsT=m_codes[:, 2 * P * m : 2 * P * (m + 1)].bitcast(E2M1),
-                        lhsT_scale=m_plane[:, P * m : P * (m + 1)],
-                        rhs=z_codes[n][:].bitcast(E4M3),
-                        rhs_scale=z_plane[n][:],
-                        start=True,
-                        stop=True,
-                    )
 
         def respond(n):
             width = Q * len(turned(n))
@@ -343,23 +331,21 @@ def tile_orchestra_bleed_mix_t2_kernel(
                     sheet = take_sheet()
                     scaled.setdefault(n, []).append(sheet)
                 scaled[n, k] = sheet[:, start : start + width]
-                b = 2 * (n % 4) + k
-                nc.scalar.activation(
-                    out=scaled[n, k], in_=bank_of["mix", n, k], func=COPY, scale=resp_col[:, b : b + 1]
-                )
+            step = Q if n == QUARTERS - 1 else W
+            for c0 in range(0, width, step):
+                for k in range(2):
+                    b = 2 * (n % 4) + k
+                    nc.scalar.activation(
+                        out=scaled[n, k][:, c0 : c0 + min(step, width)],
+                        in_=bank_of["mix", n, k][:, c0 : c0 + min(step, width)],
+                        func=COPY,
+                        scale=resp_col[:, b : b + 1],
+                    )
 
-        def respond_unturned(n):
-            for h in unturned(n):
-                unrecorded[n, h] = take_sheet()
-                nc.vector.tensor_tensor(
-                    out=unrecorded[n, h][:].rearrange("p (m f) -> p m f", m=2),
-                    in0=bank_of["unturned", n, h][:].rearrange("p (m f) -> p m f", m=2),
-                    in1=resp_all[:, Q * (n % 4) : Q * (n % 4 + 1)].unsqueeze(1).to_broadcast([P, 2, Q]),
-                    op=MULT,
-                )
-
-        def turn_back(n):
+        def turn_back(n, *hs):
             for i, h in enumerate(turned(n)):
+                if (hs and h not in hs) or ("back", n, h) in bank_of:
+                    continue
                 bank_of["back", n, h] = next_bank()
                 for dm in range(2):
                     for k in range(2):
@@ -368,11 +354,12 @@ def tile_orchestra_bleed_mix_t2_kernel(
                             scaled[n, k][:, P * (2 * i + dm) : P * (2 * i + dm + 1)],
                             ident[:],
                         )
-            idle_sheets.extend(scaled.get(n, []))
+            if all(("back", n, h) in bank_of for h in turned(n)):
+                idle_sheets.extend(scaled.pop(n, []))
 
-        def copy_back(n):
-            for h in range(2):
-                if way(n)[h] == TURNED_GPSIMD:
+        def copy_back(n, *hs):
+            for h in hs or range(2):
+                if way(n)[h] == TURNED_GPSIMD and (n, h) not in unrecorded:
                     unrecorded[n, h] = take_sheet()
                     nc.scalar.copy(out=unrecorded[n, h][:], in_=bank_of["back", n, h][:])
 
@@ -382,13 +369,13 @@ def tile_orchestra_bleed_mix_t2_kernel(
             engine.tensor_tensor(
                 out=result,
                 in0=first.rearrange("p (m f) -> p m f", m=groups),
-                in1=raw[n // 2][:, m : m + groups, Q * (n % 2) : Q * (n % 2 + 1)],
+                in1=recs[r][:, m : m + groups, bins],
                 op=ADD,
             )
             return out.rearrange("(m c) r f -> c m r f", c=P)[:, m : m + groups, r, bins], result
 
-        def add_record_vector(n):
-            for h in range(2):
+        def add_record_vector(n, *hs):
+            for h in hs or range(2):
                 if way(n)[h] in (TURNED_VECTOR, UNTURNED_VECTOR):
                     first = bank_of["back", n, h] if h in turned(n) else unrecorded[n, h]
                     parts = 2 if (n, h) == (QUARTERS - 1, 1) else 1
@@ -424,9 +411,9 @@ def tile_orchestra_bleed_mix_t2_kernel(
 
         bleed_banks, turn_banks = [0, 1, 2, 3], [4, 5, 6, 7]
 
-        def early(stage, banks, n):
+        def early(stage, banks, *which):
             turns[:] = banks
-            stage(n)
+            stage(*which)
             banks[:] = turns
 
         reorder_a_codes(nc.vector.tensor_copy)
@@ -455,31 +442,37 @@ def tile_orchestra_bleed_mix_t2_kernel(
         quantise_x(4)
         quantise_x(5)
         interleave(6, "gpsimd", True)
+        interleave(7, "gpsimd")
         bleed(2)
         early(bleed_matmuls, bleed_banks, 4)
         early(turn_y, turn_banks, 1)
         gather_y(0)
         round_y(2)
+        widen_resp()
         bleed(3)
+        bleed_banks[:2] = bleed_banks[1::-1]
+        early(bleed_matmuls, bleed_banks, 5, 0, 1)
         early(turn_y, turn_banks, 2)
-        early(bleed_matmuls, bleed_banks, 5)
+        early(turn_resp, turn_banks)
+        early(bleed_matmuls, bleed_banks, 5, 1, 2)
         round_y(3)
         early(turn_y, turn_banks, 3)
+        keep_resp()
         for n in range(1, 4):
             gather_y(n)
-        quantise_y(0)
-        quantise_x(6)
-        interleave(7, "gpsimd", True)
         bleed(4)
-        bleed(5)
+        quantise_x(6)
         quantise_x(7)
-        turns[:] = bleed_banks + turn_banks
-        bleed_matmuls(6)
+        quantise_y(0)
+        interleave(8, "gpsimd", True, 0, P)
+        early(bleed_matmuls, bleed_banks, 6)
+        bleed(5)
+        early(bleed_matmuls, bleed_banks, 7)
+        turns[:] = turn_banks + bleed_banks
         for n in range(1, 4):
             quantise_y(n)
-        interleave(8, "gpsimd", True)
-        interleave(9, "scalar")
-        widen_resp()
+        interleave(9, "gpsimd", True)
+        interleave(8, "scalar", False, P, Q)
         round_y(4)
         round_y(5)
         for n in range(LEAK_LAG):
@@ -487,34 +480,32 @@ def tile_orchestra_bleed_mix_t2_kernel(
 
         for n in range(LEAK_LAG, QUARTERS + BACK_LAG + 1):
             first = n == LEAK_LAG
-            if not first:
+            if n > LEAK_LAG + 1:
                 at(bleed_matmuls, n)
             at(leak_matmuls, n - LEAK_LAG)
-            at(mix_matmuls, n - MIX_LAG)
+            if n == LEAK_LAG + 1:
+                turn_y(n - 2)
+                gather_y(n - 2)
             at(bleed, n)
+            at(mix_matmuls, n - MIX_LAG)
             at(load_rec, n)
             if first:
                 turn_y(n - 2)
-                turn_resp()
                 gather_y(n - 2)
             at(round_y, n)
             at(respond, n - MIX_LAG)
-            if n == LEAK_LAG + 1:
-                turn_y(n - 2)
             if not first:
                 at(turn_y, n - 1)
             at(turn_back, n - BACK_LAG)
             at(leak, n - LEAK_LAG)
-            at(respond_unturned, n - MIX_LAG)
             if first:
                 quantise_x(n + X_LEAD - 1)
                 quantise_z(0)
                 quantise_x(n + X_LEAD)
             else:
-                if n in (LEAK_LAG + 1, LEAK_LAG + 2):
+                if n == LEAK_LAG + 1:
                     quantise_y(n - 3)
-                if n != LEAK_LAG + 1:
-                    at(quantise_y, n - 2)
+                at(quantise_y, n - 2)
                 at(quantise_x, n + X_LEAD)
                 at(quantise_z, n - LEAK_LAG)
             for m, kind in ((n - BACK_LAG - 1, TURNED_GPSIMD), (n - MIX_LAG, UNTURNED_GPSIMD)):
@@ -530,8 +521,6 @@ def tile_orchestra_bleed_mix_t2_kernel(
                 add_record_gpsimd(groups, tie)
                 tie = False
                 left -= groups
-            if n == LEAK_LAG + 1:
-                gather_y(n - 2)
             if not first:
                 at(gather_y, n - 1)
             at(copy_back, n - BACK_LAG)

@@ -215,8 +215,8 @@ def tile_orchestra_bleed_mix_t2_kernel(
             if n not in y_bf16:
                 y_bf16[n] = take_sheet()
             nc.scalar.copy(
-                out=y_bf16[n][:].bitcast(BF16)[:, W * t0 : W * t1].rearrange("p (t h w e) -> p t h w e", w=P, h=2, e=2),
-                in_=y[u][:, 2 * j + t0 : 2 * j + t1, :].rearrange("p t (w h e) -> p t h w e", h=2, e=2),
+                out=y_bf16[n][:].bitcast(BF16)[:, W * t0 : W * t1].rearrange("p (t h w e) -> p t w h e", w=P, h=2, e=2),
+                in_=y[u][:, 2 * j + t0 : 2 * j + t1, :].rearrange("p t (w h e) -> p t w h e", h=2, e=2),
             )
 
         def turn_y(n):
@@ -270,9 +270,9 @@ def tile_orchestra_bleed_mix_t2_kernel(
                 z_half = z[n][:, Q * k : Q * (k + 1)].bitcast(BF16)
                 bins = slice(Q * j + P * k, Q * j + P * (k + 1))
                 nc.vector.tensor_tensor(
-                    out=z_half.rearrange("p (c i t) -> p c t i", i=4, t=4),
-                    in0=bank_of["leak", n, k][:].rearrange("p (t c i) -> p c t i", t=4, i=4),
-                    in1=y[u][:, :, bins].rearrange("p t (c i) -> p c t i", i=4),
+                    out=z_half.rearrange("p (c i t) -> p c t i", i=8, t=4),
+                    in0=bank_of["leak", n, k][:].rearrange("p (t c i) -> p c t i", t=4, i=8),
+                    in1=y[u][:, :, bins].rearrange("p t (c i) -> p c t i", i=8),
                     op=ADD,
                 )
 
@@ -426,9 +426,10 @@ def tile_orchestra_bleed_mix_t2_kernel(
         early(bleed_matmuls, bleed_banks, 0)
         early(bleed_matmuls, bleed_banks, 1)
         interleave(2, "vector")
-        interleave(3, "scalar")
-        quantise_x(2)
+        interleave(3, "vector", False, 0, Q // 4)
+        interleave(3, "scalar", False, Q // 4, Q)
         nc.vector.tensor_copy(out=damp_col[:], in_=damp_arrived[:])
+        quantise_x(2)
         quantise_x(3)
         interleave(4, "scalar")
         interleave(5, "gpsimd", True)

@@ -35,6 +35,7 @@ X_LEAD = 3
 TURNED_VECTOR, TURNED_GPSIMD, UNTURNED_GPSIMD, UNTURNED_VECTOR = "a", "g", "b", "c"
 WAYS = "ag ag ag ag ag ag ag ag ag ag ag ag ag aa aa aa".split()
 GA = {}
+SPLIT = 16
 GB = {9:192,10:192,11:192}
 
 
@@ -214,10 +215,13 @@ def tile_orchestra_bleed_mix_t2_kernel(
             u, j = divmod(n, 2)
             if n not in y_bf16:
                 y_bf16[n] = take_sheet()
-            nc.scalar.copy(
-                out=y_bf16[n][:].bitcast(BF16)[:, W * t0 : W * t1].rearrange("p (t h w e) -> p t w h e", w=P, h=2, e=2),
-                in_=y[u][:, 2 * j + t0 : 2 * j + t1, :].rearrange("p t (w h e) -> p t w h e", h=2, e=2),
-            )
+            step = 1 if n < SPLIT else 2
+            for t in range(0, 2, step):
+                rounded = y_bf16[n][:].bitcast(BF16)[:, W * t : W * (t + step)]
+                nc.scalar.copy(
+                    out=rounded.rearrange("p (t h w e) -> p t w h e", w=P, h=2, e=2),
+                    in_=y[u][:, 2 * j + t : 2 * j + t + step, :].rearrange("p t (w h e) -> p t w h e", h=2, e=2),
+                )
 
         def turn_y(n):
             bank_of["turn", n] = next_bank()

@@ -33,7 +33,7 @@ BACK_LAG = LEAK_LAG + 2
 X_LEAD = 3
 
 TURNED_VECTOR, TURNED_GPSIMD, UNTURNED_GPSIMD, UNTURNED_VECTOR = "a", "g", "b", "c"
-WAYS = "ag ag ag ag ag ag ag ag ag ag ag ag ag aa aa aa".split()
+WAYS = "ag ag ag ag ag ag ag ag ag ag ag ag aa aa aa aa".split()
 GA = {}
 SPLIT = 16
 GB = {9:192,10:192,11:192}
@@ -125,9 +125,9 @@ def tile_orchestra_bleed_mix_t2_kernel(
         load_x(2, 1)
         load_x(3, 1)
         nc.sync.dma_start(out=resp_rows[0 : F // P, :], in_=resp.rearrange("(b q) -> b q", q=P))
-        load_x(4, 2)
         nc.sync.dma_start(out=as_int32(l_codes[:]), in_=as_int32(l_words.rearrange("g p n -> p g n")))
         load_scales(l_plane, l_scales)
+        load_x(4, 2)
         nc.sync.dma_start(out=as_int32(m_codes[:]), in_=as_int32(m_words[0]))
         load_scales(m_plane, m_scales)
         load_x(6, 2)

@@ -98,7 +98,16 @@ def tile_orchestra_bleed_mix_t2_kernel(
             bins = slice(W * g, W * (g + halves))
             nc.sync.dma_start(out=loaded, in_=x.rearrange("(p t) r f -> p t r f", t=4)[:, :, r, bins])
             for i in range(halves):
-                raw[u + i] = loaded[:, :, W * i : W * (i + 1)]
+                raw[u + i] = loaded[:, :, W * i : W * (i + 1)].rearrange("p t (j f) -> p t j f", j=2)
+
+        def load_first_quarters():
+            frames[0] = keep.tile([P, 4 * F], BF16, align_bytes=64, name="frame0")
+            for j in range(2):
+                nc.sync.dma_start(
+                    out=frames[0][:, 4 * Q * j : 4 * Q * (j + 1)].rearrange("p (t f) -> p t f", t=4),
+                    in_=x.rearrange("(p t) r f -> p t r f", t=4)[:, :, 0, Q * j : Q * (j + 1)],
+                )
+            raw[0] = frames[0][:, 0 : 4 * W].rearrange("p (j t f) -> p t j f", j=2, t=4)
 
         def load_rec(n):
             r = n // 4
@@ -118,7 +127,7 @@ def tile_orchestra_bleed_mix_t2_kernel(
                     )
 
         nc.sync.dma_start(out=as_int32(a_arrived[:]), in_=as_int32(a_words[0]))
-        load_x(0, 1)
+        load_first_quarters()
         load_scales(a_scales_arrived, a_scales)
         load_x(1, 1)
         nc.sync.dma_start(out=damp_arrived[:], in_=damp.rearrange("(p t) -> p t", t=4))
@@ -159,7 +168,7 @@ def tile_orchestra_bleed_mix_t2_kernel(
             if n not in grouped:
                 grouped[n] = take_sheet(behind_quantising)
             out_ap = grouped[n][:].bitcast(BF16)[:, 4 * f0 : 4 * f1].rearrange("p (f t) -> p f t", t=4)
-            in_ap = raw[n // 2][:, :, Q * (n % 2) + f0 : Q * (n % 2) + f1]
+            in_ap = raw[n // 2][:, :, n % 2, f0:f1]
             if engine == "gpsimd":
                 nc.gpsimd.tensor_scalar(
                     out=out_ap, in0=in_ap.rearrange("p t f -> p f t"), scalar1=1.0, scalar2=0.0, op0=MULT, op1=ADD
@@ -203,10 +212,10 @@ def tile_orchestra_bleed_mix_t2_kernel(
                 y[u] = work.tile([P, 4, W], F32, align_bytes=64, name="y", bufs=5)
             for t in range(2 * j + t0, 2 * j + t1):
                 nc.vector.scalar_tensor_tensor(
-                    out=y[u][:, t, :],
-                    in0=bank_of["bleed", u, t][:],
+                    out=y[u][:, t, :].rearrange("p (j f) -> p j f", j=2),
+                    in0=bank_of["bleed", u, t][:].rearrange("p (j f) -> p j f", j=2),
                     scalar=damp_col[:, t : t + 1],
-                    in1=raw[u][:, t, :],
+                    in1=raw[u][:, t, :, :],
                     op0=MULT,
                     op1=ADD,
                 )

@@ -283,9 +283,9 @@ def tile_orchestra_bleed_mix_t2_kernel(
                 z_half = z[n][:, Q * k : Q * (k + 1)].bitcast(BF16)
                 bins = slice(Q * j + P * k, Q * j + P * (k + 1))
                 nc.vector.tensor_tensor(
-                    out=z_half.rearrange("p (c i t) -> p c t i", i=8, t=4),
-                    in0=bank_of["leak", n, k][:].rearrange("p (t c i) -> p c t i", t=4, i=8),
-                    in1=y[u][:, :, bins].rearrange("p t (c i) -> p c t i", i=8),
+                    out=z_half.rearrange("p (c i t) -> p c t i", i=2, t=4),
+                    in0=bank_of["leak", n, k][:].rearrange("p (t c i) -> p c t i", t=4, i=2),
+                    in1=y[u][:, :, bins].rearrange("p t (c i) -> p c t i", i=2),
                     op=ADD,
                 )
 

from contextlib import ExitStack

import concourse.mybir as mybir
from concourse.masks import make_identity

F32 = mybir.dt.float32
BF16 = mybir.dt.bfloat16
U32 = mybir.dt.uint32
I32 = mybir.dt.int32
U16 = mybir.dt.uint16
U8 = mybir.dt.uint8
E4M3 = mybir.dt.float8_e4m3fn_x4
E2M1 = mybir.dt.float4_e2m1fn_x4
ADD = mybir.AluOpType.add
MULT = mybir.AluOpType.mult
COPY = mybir.ActivationFunctionType.Copy

S, T, F, C = 512, 4, 1024, 512
P = 128
W = 512
Q = 256
HALF_FRAMES = 2 * T
QUARTERS = 4 * T
FLOPS = 2 * (2 * S * S * T * F + S * T * F * F)

BANKS = 8
SHEETS = 64
RESTING = 6

LEAK_LAG = 6
MIX_LAG = LEAK_LAG + 1
BACK_LAG = LEAK_LAG + 2
X_LEAD = 3

TURNED_VECTOR, TURNED_GPSIMD, UNTURNED_GPSIMD, UNTURNED_VECTOR = "a", "g", "b", "c"
WAYS = "ag ag ag ag ag ag ag ag ag ag ag ag aa aa aa aa".split()
GA = {}
SPLIT = 16
GB = {9:192,10:192,11:192}


def way(n):
    return WAYS[n]


def tile_orchestra_bleed_mix_t2_kernel(
    tc, x, a_words, a_scales, l_words, l_scales, m_words, m_scales, damp, resp, rec, out
):
    nc = tc.nc
    with ExitStack() as ctx:
        keep = ctx.enter_context(tc.tile_pool(name="keep", bufs=1))
        work = ctx.enter_context(tc.tile_pool(name="work", bufs=2))
        psum = ctx.enter_context(tc.psum_pool(name="psum", bufs=1))
        ctx.enter_context(tc.manual_schedule())

        a_arrived = keep.tile([P, 2 * S], U8, align_bytes=64, name="a_arrived")
        a_scales_arrived = keep.tile([P, S], U8, align_bytes=64, name="a_scales_arrived")
        a_codes = keep.tile([P, 2 * S], U8, align_bytes=64, name="a_codes")
        a_plane = keep.tile([P, S], U8, align_bytes=64, name="a_plane")
        l_codes = keep.tile([P, 2, 2 * F], U8, align_bytes=64, name="l_codes")
        l_plane = keep.tile([P, 2, F], U8, align_bytes=64, name="l_plane")
        m_codes = keep.tile([P, 2 * C], U8, align_bytes=64, name="m_codes")
        m_plane = keep.tile([P, C], U8, align_bytes=64, name="m_plane")
        damp_arrived = keep.tile([P, 4], BF16, name="damp_arrived")
        damp_col = keep.tile([P, 4], F32, name="damp_col")
        resp_rows = keep.tile([P, P], BF16, align_bytes=64, name="resp_rows")
        resp_wide = keep.tile([P, P], F32, align_bytes=64, name="resp_wide")
        resp_col = keep.tile([P, F // P], F32, name="resp_col")
        ident = keep.tile([P, P], F32, align_bytes=64, name="ident")

        idle_sheets, spare_sheets = [], []
        for i in range(SHEETS):
            sheet = keep.tile([P, W], F32, align_bytes=64, name="sheet%d" % i)
            spare_sheets.append(sheet)

        def take_sheet(behind_quantising=False):
            if behind_quantising:
                return idle_sheets.pop()
            return idle_sheets.pop(0) if len(idle_sheets) > RESTING else spare_sheets.pop(0)

        def as_int32(ap):
            return ap.bitcast(I32)

        nc.vector.memset(as_int32(a_scales_arrived[:]), 0)
        nc.vector.memset(ident[:], 0.0)
        nc.vector.memset(as_int32(l_plane[:]), 0)
        nc.vector.memset(as_int32(m_plane[:]), 0)
        nc.vector.memset(resp_rows[:], 0.0)
        make_identity(nc, ident[:], nomemset=True)

        frames, raw, recs = {}, {}, {}

        def load_x(u, halves):
            r, g = divmod(u, 2)
            if g == 0:
                frames[r] = keep.tile([P, 4 * F], BF16, align_bytes=64, name="frame%d" % r)
            loaded = frames[r][:, 4 * W * g : 4 * W * (g + halves)].rearrange("p (t f) -> p t f", t=4)
            bins = slice(W * g, W * (g + halves))
            nc.sync.dma_start(out=loaded, in_=x.rearrange("(p t) r f -> p t r f", t=4)[:, :, r, bins])
            for i in range(halves):
                raw[u + i] = loaded[:, :, W * i : W * (i + 1)].rearrange("p t (j f) -> p t j f", j=2)

        def load_first_quarters():
            frames[0] = keep.tile([P, 4 * F], BF16, align_bytes=64, name="frame0")
            for j in range(2):
                nc.sync.dma_start(
                    out=frames[0][:, 4 * Q * j : 4 * Q * (j + 1)].rearrange("p (t f) -> p t f", t=4),
                    in_=x.rearrange("(p t) r f -> p t r f", t=4)[:, :, 0, Q * j : Q * (j + 1)],
                )
            raw[0] = frames[0][:, 0 : 4 * W].rearrange("p (j t f) -> p t j f", j=2, t=4)

        def load_rec(n):
            r = n // 4
            if n % 4 == 3:
                recs[r] = frames[r][:].rearrange("p (m f) -> p m f", m=C // P)
                nc.sync.dma_start(out=recs[r], in_=rec.rearrange("(m c) r f -> c m r f", c=P)[:, :, r, :])

        def load_scales(plane, scales, queue=nc.sync):
            for q in range(4):
                rows = slice(32 * q, 32 * q + 4)
                if scales.shape[0] == 1:
                    queue.dma_start(out=as_int32(plane[rows, :]), in_=as_int32(scales[0, 4 * q : 4 * q + 4, :]))
                else:
                    nc.sync.dma_start(
                        out=as_int32(plane[rows, :, :]),
                        in_=as_int32(scales[:, 4 * q : 4 * q + 4, :].rearrange("g q n -> q g n")),
                    )

        nc.sync.dma_start(out=as_int32(a_arrived[:]), in_=as_int32(a_words[0]))
        load_first_quarters()
        load_scales(a_scales_arrived, a_scales)
        load_x(1, 1)
        nc.sync.dma_start(out=damp_arrived[:], in_=damp.rearrange("(p t) -> p t", t=4))
        load_x(2, 1)
        load_x(3, 1)
        nc.sync.dma_start(out=resp_rows[0 : F // P, :], in_=resp.rearrange("(b q) -> b q", q=P))
        nc.sync.dma_start(out=as_int32(l_codes[:]), in_=as_int32(l_words.rearrange("g p n -> p g n")))
        load_scales(l_plane, l_scales)
        load_x(4, 2)
        nc.sync.dma_start(out=as_int32(m_codes[:]), in_=as_int32(m_words[0]))
        load_scales(m_plane, m_scales)
        load_x(6, 2)

        def reorder_a_codes(copy):
            copy(
                out=a_codes[:].bitcast(U16).rearrange("p (t m) -> p t m", t=4),
                in_=a_arrived[:].bitcast(U16).rearrange("p (m t) -> p t m", t=4),
            )

        def reorder_a_scales():
            nc.vector.tensor_copy(
                out=a_plane[:].rearrange("p (t m) -> p t m", t=4),
                in_=a_scales_arrived[:].rearrange("p (m t) -> p t m", t=4),
            )

        grouped, x_codes, x_plane, y, y_bf16, y_turned, y_codes, y_plane = {}, {}, {}, {}, {}, {}, {}, {}
        unstored, waiting = [], []
        z, z_codes, z_plane, scaled, unrecorded, bank_of = {}, {}, {}, {}, {}, {}

        turns = []

        def next_bank():
            i = turns.pop(0)
            turns.append(i)
            return psum.tile([P, W], F32, name="bank%d" % i)

        def interleave(n, engine, behind_quantising=False, f0=0, f1=Q):
            if n not in grouped:
                grouped[n] = take_sheet(behind_quantising)
            out_ap = grouped[n][:].bitcast(BF16)[:, 4 * f0 : 4 * f1].rearrange("p (f t) -> p f t", t=4)
            in_ap = raw[n // 2][:, :, n % 2, f0:f1]
            if engine == "gpsimd":
                nc.gpsimd.tensor_scalar(
                    out=out_ap, in0=in_ap.rearrange("p t f -> p f t"), scalar1=1.0, scalar2=0.0, op0=MULT, op1=ADD
                )
            else:
                copy = nc.vector.tensor_copy if engine == "vector" else nc.scalar.copy
                copy(
                    out=out_ap.rearrange("p (c i) t -> p c t i", i=4),
                    in_=in_ap.rearrange("p t (c i) -> p c t i", i=4),
                )

        def quantise_x(n):
            u, j = divmod(n, 2)
            if j == 0:
                x_codes[u] = work.tile([P, W], U32, align_bytes=64, name="x_codes", bufs=3)
                x_plane[u] = work.tile([P, W], U8, align_bytes=64, name="x_plane", bufs=3)
            nc.vector.quantize_mx(
                out=x_codes[u][:, Q * j : Q * (j + 1)].bitcast(E4M3),
                scales=x_plane[u][:, Q * j : Q * (j + 1)],
                in_=grouped[n][:].bitcast(BF16),
            )
            idle_sheets.append(grouped[n])

        def bleed_matmuls(n, t0=0, t1=2):
            u, j = divmod(n, 2)
            for t in range(2 * j + t0, 2 * j + t1):
                bank_of["bleed", u, t] = next_bank()
                nc.tensor.matmul_mx(
                    out=bank_of["bleed", u, t][:],
                    lhsT=a_codes[:, 2 * P * t : 2 * P * (t + 1)].bitcast(E2M1),
                    lhsT_scale=a_plane[:, P * t : P * (t + 1)],
                    rhs=x_codes[u][:].bitcast(E4M3),
                    rhs_scale=x_plane[u][:],
                    start=True,
                    stop=True,
                )

        def bleed(n, t0=0, t1=2):
            u, j = divmod(n, 2)
            if u not in y:
                y[u] = work.tile([P, 4, W], F32, align_bytes=64, name="y", bufs=5)
            for t in range(2 * j + t0, 2 * j + t1):
                nc.vector.scalar_tensor_tensor(
                    out=y[u][:, t, :].rearrange("p (j f) -> p j f", j=2),
                    in0=bank_of["bleed", u, t][:].rearrange("p (j f) -> p j f", j=2),
                    scalar=damp_col[:, t : t + 1],
                    in1=raw[u][:, t, :, :],
                    op0=MULT,
                    op1=ADD,
                )

        def round_y(n, t0=0, t1=2):
            u, j = divmod(n, 2)
            if n not in y_bf16:
                y_bf16[n] = take_sheet()
            step = 1 if n < SPLIT else 2
            for t in range(0, 2, step):
                rounded = y_bf16[n][:].bitcast(BF16)[:, W * t : W * (t + step)]
                nc.scalar.copy(
                    out=rounded.rearrange("p (t h w e) -> p t w h e", w=P, h=2, e=2),
                    in_=y[u][:, 2 * j + t : 2 * j + t + step, :].rearrange("p t (w h e) -> p t w h e", h=2, e=2),
                )

        def turn_y(n):
            bank_of["turn", n] = next_bank()
            for i in range(4):
                nc.tensor.transpose(
                    bank_of["turn", n][:, P * i : P * (i + 1)], y_bf16[n][:, P * i : P * (i + 1)], ident[:]
                )
            idle_sheets.append(y_bf16[n])

        def gather_y(n):
            y_turned[n] = take_sheet()
            nc.scalar.copy(
                out=y_turned[n][:].rearrange("w (t p h) -> w t p h", t=2, h=2),
                in_=bank_of["turn", n][:].rearrange("w (t h p) -> w t p h", t=2, h=2),
            )

        def quantise_y(n):
            u, j = divmod(n, 2)
            if j == 0:
                y_codes[u] = work.tile([P, S], U32, align_bytes=64, name="y_codes", bufs=4)
                y_plane[u] = work.tile([P, S], U8, align_bytes=64, name="y_plane", bufs=4)
            nc.vector.quantize_mx(
                out=y_codes[u][:, Q * j : Q * (j + 1)].bitcast(E4M3),
                scales=y_plane[u][:, Q * j : Q * (j + 1)],
                in_=y_turned[n][:].bitcast(BF16),
            )
            idle_sheets.append(y_turned[n])

        def leak_matmuls(n):
            r = n // 4
            for k in range(2):
                b = 2 * (n % 4) + k
                bank_of["leak", n, k] = next_bank()
                for t in range(4):
                    for g in range(2):
                        nc.tensor.matmul_mx(
                            out=bank_of["leak", n, k][:, P * t : P * (t + 1)],
                            lhsT=y_codes[2 * r + g][:, P * t : P * (t + 1)].bitcast(E4M3),
                            lhsT_scale=y_plane[2 * r + g][:, P * t : P * (t + 1)],
                            rhs=l_codes[:, g, 2 * P * b : 2 * P * (b + 1)].bitcast(E2M1),
                            rhs_scale=l_plane[:, g, P * b : P * (b + 1)],
                            start=(g == 0),
                            stop=(g == 1),
                        )

        def leak(n):
            u, j = divmod(n, 2)
            z[n] = take_sheet()
            for k in range(2):
                z_half = z[n][:, Q * k : Q * (k + 1)].bitcast(BF16)
                bins = slice(Q * j + P * k, Q * j + P * (k + 1))
                nc.vector.tensor_tensor(
                    out=z_half.rearrange("p (c i t) -> p c t i", i=2, t=4),
                    in0=bank_of["leak", n, k][:].rearrange("p (t c i) -> p c t i", t=4, i=2),
                    in1=y[u][:, :, bins].rearrange("p t (c i) -> p c t i", i=2),
                    op=ADD,
                )

        def quantise_z(n):
            z_codes[n] = work.tile([P, Q], U32, align_bytes=64, name="z_codes", bufs=3)
            z_plane[n] = work.tile([P, Q], U8, align_bytes=64, name="z_plane", bufs=3)
            width = P if n == QUARTERS - 1 else Q
            for f0 in range(0, Q, width):
                nc.vector.quantize_mx(
                    out=z_codes[n][:, f0 : f0 + width].bitcast(E4M3),
                    scales=z_plane[n][:, f0 : f0 + width],
                    in_=z[n][:, 2 * f0 : 2 * (f0 + width)].bitcast(BF16),
                )
            idle_sheets.append(z[n])

        def widen_resp():
            nc.scalar.copy(out=resp_wide[:], in_=resp_rows[:])

        def turn_resp():
            bank = next_bank()
            nc.tensor.transpose(bank[:, 0:P], resp_wide[:], ident[:])
            bank_of["resp"] = bank

        def keep_resp():
            nc.scalar.copy(out=resp_col[:], in_=bank_of["resp"][:, 0 : F // P])

        def turned(n):
            return [h for h in range(2) if way(n)[h] in (TURNED_VECTOR, TURNED_GPSIMD)]

        def unturned(n):
            return [h for h in range(2) if h not in turned(n)]

        def mix_matmuls(n):
            width = Q * len(turned(n))
            for k in range(2 if width else 0):
                c0 = Q * turned(n)[0]
                start = k * width % W
                if start == 0:
                    bank = next_bank()
                bank_of["mix", n, k] = bank[:, start : start + width]
                nc.tensor.matmul_mx(
                    out=bank_of["mix", n, k],
                    lhsT=z_codes[n][:, P * k : P * (k + 1)].bitcast(E4M3),
                    lhsT_scale=z_plane[n][:, P * k : P * (k + 1)],
                    rhs=m_codes[:, 2 * c0 : 2 * (c0 + width)].bitcast(E2M1),
                    rhs_scale=m_plane[:, c0 : c0 + width],
                    start=True,
                    stop=True,
                )

        def respond(n):
            width = Q * len(turned(n))
            for k in range(2 if width else 0):
                start = k * width % W
                if start == 0:
                    sheet = take_sheet()
                    scaled.setdefault(n, []).append(sheet)
                scaled[n, k] = sheet[:, start : start + width]
            step = Q if n == QUARTERS - 1 else W
            for c0 in range(0, width, step):
                for k in range(2):
                    b = 2 * (n % 4) + k
                    nc.scalar.activation(
                        out=scaled[n, k][:, c0 : c0 + min(step, width)],
                        in_=bank_of["mix", n, k][:, c0 : c0 + min(step, width)],
                        func=COPY,
                        scale=resp_col[:, b : b + 1],
                    )

        def turn_back(n, *hs):
            for i, h in enumerate(turned(n)):
                if (hs and h not in hs) or ("back", n, h) in bank_of:
                    continue
                bank_of["back", n, h] = next_bank()
                for dm in range(2):
                    for k in range(2):
                        nc.tensor.transpose(
                            bank_of["back", n, h][:, Q * dm + P * k : Q * dm + P * (k + 1)],
                            scaled[n, k][:, P * (2 * i + dm) : P * (2 * i + dm + 1)],
                            ident[:],
                        )
            if all(("back", n, h) in bank_of for h in turned(n)):
                idle_sheets.extend(scaled.pop(n, []))

        def copy_back(n, *hs):
            for h in hs or range(2):
                if way(n)[h] == TURNED_GPSIMD and (n, h) not in unrecorded:
                    unrecorded[n, h] = take_sheet()
                    nc.scalar.copy(out=unrecorded[n, h][:], in_=bank_of["back", n, h][:])

        def add_record(engine, n, m, groups, first, result):
            r, bins = n // 4, slice(Q * (n % 4), Q * (n % 4 + 1))
            result = result.rearrange("p (m f) -> p m f", m=groups)
            engine.tensor_tensor(
                out=result,
                in0=first.rearrange("p (m f) -> p m f", m=groups),
                in1=recs[r][:, m : m + groups, bins],
                op=ADD,
            )
            return out.rearrange("(m c) r f -> c m r f", c=P)[:, m : m + groups, r, bins], result

        def add_record_vector(n, *hs):
            for h in hs or range(2):
                if way(n)[h] in (TURNED_VECTOR, UNTURNED_VECTOR):
                    first = bank_of["back", n, h] if h in turned(n) else unrecorded[n, h]
                    parts = 2 if (n, h) == (QUARTERS - 1, 1) else 1
                    for dm in range(parts):
                        result = take_sheet()
                        cols = slice(W // parts * dm, W // parts * (dm + 1))
                        m = 2 * h + dm
                        target, block = add_record(nc.vector, n, m, 2 // parts, first[:, cols], result[:, 0 : W // parts])
                        queue = nc.scalar if n == QUARTERS - 1 and m != 2 else nc.sync
                        queue.dma_start(out=target, in_=block)
                        spare_sheets.append(result)
                    if h in unturned(n):
                        idle_sheets.append(unrecorded[n, h])

        def add_record_gpsimd(groups, behind_quantising):
            n, m = waiting[0]
            waiting[:groups] = []
            result = take_sheet(behind_quantising)
            first = unrecorded[n, m // 2][:, Q * (m % 2) : Q * (m % 2 + groups)]
            unstored.append((result, add_record(nc.gpsimd, n, m, groups, first, result[:, 0 : Q * groups])))
            if (m + groups) % 2 == 0:
                spare_sheets.append(unrecorded[n, m // 2])

        def store_gpsimd():
            for result, (target, block) in unstored:
                nc.sync.dma_start(out=target, in_=block)
                spare_sheets.append(result)
            unstored.clear()

        def at(stage, n, *rest):
            if 0 <= n < QUARTERS:
                stage(n, *rest)

        bleed_banks, turn_banks = [0, 1, 2, 3], [4, 5, 6, 7]

        def early(stage, banks, *which):
            turns[:] = banks
            stage(*which)
            banks[:] = turns

        reorder_a_codes(nc.vector.tensor_copy)
        interleave(0, "vector")
        interleave(1, "vector", False, 0, Q // 2)
        interleave(1, "scalar", False, Q // 2, Q)
        reorder_a_scales()
        quantise_x(0)
        quantise_x(1)
        early(bleed_matmuls, bleed_banks, 0)
        early(bleed_matmuls, bleed_banks, 1)
        interleave(2, "vector")
        interleave(3, "vector", False, 0, Q // 4)
        interleave(3, "scalar", False, Q // 4, Q)
        nc.vector.tensor_copy(out=damp_col[:], in_=damp_arrived[:])
        quantise_x(2)
        quantise_x(3)
        interleave(4, "scalar")
        interleave(5, "gpsimd", True)
        bleed(0)
        early(bleed_matmuls, bleed_banks, 2)
        round_y(0)
        bleed(1)
        early(bleed_matmuls, bleed_banks, 3)
        round_y(1)
        early(turn_y, turn_banks, 0)
        quantise_x(4)
        quantise_x(5)
        interleave(6, "gpsimd", True)
        interleave(7, "gpsimd")
        bleed(2)
        early(bleed_matmuls, bleed_banks, 4)
        early(turn_y, turn_banks, 1)
        gather_y(0)
        round_y(2)
        widen_resp()
        bleed(3)
        bleed_banks[:2] = bleed_banks[1::-1]
        early(bleed_matmuls, bleed_banks, 5, 0, 1)
        early(turn_y, turn_banks, 2)
        early(turn_resp, turn_banks)
        early(bleed_matmuls, bleed_banks, 5, 1, 2)
        round_y(3)
        early(turn_y, turn_banks, 3)
        keep_resp()
        for n in range(1, 4):
            gather_y(n)
        bleed(4)
        quantise_x(6)
        quantise_x(7)
        quantise_y(0)
        interleave(8, "gpsimd", True, 0, P)
        early(bleed_matmuls, bleed_banks, 6)
        bleed(5)
        early(bleed_matmuls, bleed_banks, 7)
        turns[:] = turn_banks + bleed_banks
        for n in range(1, 4):
            quantise_y(n)
        interleave(9, "gpsimd", True)
        interleave(8, "scalar", False, P, Q)
        round_y(4)
        round_y(5)
        for n in range(LEAK_LAG):
            load_rec(n)

        for n in range(LEAK_LAG, QUARTERS + BACK_LAG + 1):
            first = n == LEAK_LAG
            if n > LEAK_LAG + 1:
                at(bleed_matmuls, n)
            at(leak_matmuls, n - LEAK_LAG)
            if n == LEAK_LAG + 1:
                turn_y(n - 2)
                gather_y(n - 2)
            at(bleed, n)
            at(mix_matmuls, n - MIX_LAG)
            at(load_rec, n)
            if first:
                turn_y(n - 2)
                gather_y(n - 2)
            at(round_y, n)
            at(respond, n - MIX_LAG)
            if not first:
                at(turn_y, n - 1)
            at(turn_back, n - BACK_LAG)
            at(leak, n - LEAK_LAG)
            if first:
                quantise_x(n + X_LEAD - 1)
                quantise_z(0)
                quantise_x(n + X_LEAD)
            else:
                if n == LEAK_LAG + 1:
                    quantise_y(n - 3)
                at(quantise_y, n - 2)
                at(quantise_x, n + X_LEAD)
                at(quantise_z, n - LEAK_LAG)
            for m, kind in ((n - BACK_LAG - 1, TURNED_GPSIMD), (n - MIX_LAG, UNTURNED_GPSIMD)):
                if 0 <= m < QUARTERS:
                    waiting.extend((m, 2 * h + dm) for h in range(2) for dm in range(2) if way(m)[h] == kind)
            tie = True
            if n + X_LEAD + 1 < QUARTERS:
                interleave(n + X_LEAD + 1, "gpsimd", True, 0, GB.get(n, Q))
                tie = False
            left = GA.get(n, 2)
            while left and waiting:
                groups = min(left, 2 - waiting[0][1] % 2)
                add_record_gpsimd(groups, tie)
                tie = False
                left -= groups
            if not first:
                at(gather_y, n - 1)
            at(copy_back, n - BACK_LAG)
            if n in GB:
                interleave(n + X_LEAD + 1, "scalar", False, GB[n], Q)
            at(add_record_vector, n - BACK_LAG)
            store_gpsimd()
